import numpy as np, ml_dtypes
CORES = [36,164,52,180,100,228,116,244]
N = 8
import mx_ref
BF = ml_dtypes.bfloat16
def gcols(t, e):
    v = np.concatenate([t.reshape(8, 16, -1, 4), np.zeros((8, 16, 1, 4), BF)], axis=2)
    return np.ascontiguousarray(np.stack([v[g][:, e[g]] for g in range(8)])).reshape(128, -1)
def tile(rs):
    return np.stack(rs, axis=2).reshape(128, -1).astype(BF)
def cut(t, i, w=512):
    return t[:, w * i:w * i + w]
def pick(q, e):
    c = np.concatenate([q[0].reshape(128, -1, 4), np.zeros((128, 1, 4), np.uint8)], axis=1); s = np.concatenate([q[1], np.ones((16, 1), np.uint8)], axis=1)
    return (np.ascontiguousarray(c[:, e].reshape(128, -1)), np.ascontiguousarray(s[:, e]))
def join(*qs):
    return (np.concatenate([q[0] for q in qs], axis=1), np.concatenate([q[1] for q in qs], axis=1))
def put(q, e, v):
    c, s = q[0].reshape(128, -1, 4).copy(), q[1].copy(); c[:, e] = v[0].reshape(128, -1, 4); s[:, e] = v[1]
    return (c.reshape(128, -1), s)
def pk(c, s):
    return (np.ascontiguousarray(c), mx_ref.live(s))
def emit(q):
    return q[0], q[1]
def packed(v, rng):
    q = [mx_ref.quantize(np.ascontiguousarray(v[r])) for r in range(N)]
    return np.stack([a for a, b in q]), np.stack([mx_ref.plane(b, rng) for a, b in q])
def values_of_codes():
    e, c = np.zeros((128, 128, 4), np.float32), np.zeros((128, 2, 4), np.uint8)
    e[np.arange(128), np.arange(128), 0] = 1
    c[:127, :, 0] = np.arange(256).reshape(2, 128).T[:127]
    return mx_ref.matmul(mx_ref.quantize(e.reshape(128, 512).astype(BF)), (c.reshape(128, 8), np.full((16, 2), 127, np.uint8))).T.reshape(-1).astype(np.float64)
CODE_VALUE, SCALE_VALUE = values_of_codes(), 2.0 ** (np.arange(256) - 127.0)
def decode(q):
    return (CODE_VALUE[q[0]].reshape(16, 8, -1, 4) * SCALE_VALUE[q[1]][:, None, :, None] + 0.0).reshape(128, -1).astype(np.float32)
def f(rng, *shape):
    return mx_ref.flush((rng.standard_normal(shape, dtype=np.float32) * np.exp2(rng.integers(-2, 3, shape[:-1] + (1,)))).astype(BF))
def wide(rng, *shape, cols=0):
    v = rng.standard_normal(shape, dtype=np.float32) * np.exp2(rng.integers(-12, 13, shape)).astype(np.float32)
    if cols: v *= np.repeat(np.exp2(rng.integers(-cols, cols + 1, shape[:-2] + (1, shape[-1] // 4))) * (rng.random(shape[:-2] + (1, shape[-1] // 4)) > 0.0625), 4, axis=-1).astype(np.float32)
    return mx_ref.flush(v.astype(BF))
C, A, K, R = 352, 96, 160, 3
STEP = [1, 6, 7]
def order(p):
    return np.argsort(-(p[::16] + np.float32(0.0)), axis=1, kind="stable")
def gput(t, e, h):
    a, b = t.reshape(8, 16, -1, 4).copy(), h.reshape(8, 16, -1, 4)
    for g in range(8): a[g][:, e[g]] = b[g]
    return a.reshape(128, -1)
def parts(m):
    return np.repeat(np.repeat(m, 16, axis=0), 4, axis=1)
def big(v):
    v = v.astype(np.float32)
    v[np.abs(v) < np.float32(2.0 ** -16)] = 0
    return v.astype(BF)
def numbers_of(rng):
    return {"x": big(f(rng, N, 128, 4 * C)), "u": np.array(f(rng, N, 128, 512)), "v": np.array(f(rng, N, 128, 512))}
def layers(rng):
    return big(f(rng, N, 128, 2048)).reshape(N, 8, 16, 4, 8, 16, 4)
def weights(rng, w):
    c, p = packed(np.ascontiguousarray(w).reshape(N, 128, 2048), rng)
    return {"wc": c, "ws": p}
def signs(rng):
    return np.stack([rng.permutation(8) % 2 * 2.0 - 1.0 for r in range(N)])
def setup_inputs(rng):
    return {**numbers_of(rng), **weights(rng, layers(rng))}
def setup_inputs_ties(rng):
    d = numbers_of(rng)
    e = rng.permutation(N)
    x = d["x"].reshape(N, 8, 16, C, 4)
    for r in range(N):
        k = np.zeros(C, int) if r == e[0] else rng.permutation(C) % 3
        a = x[r][:, :8, :3].copy()
        a[:, :, 2] = 0
        x[r][:, :8] = a[:, :, k]
    x[e[1]] = 0
    u = d["u"].reshape(N, 8, 16, 128, 4)
    u[:, :, 8:, ::16] = 0
    w = layers(rng)
    w[:, :, 8:, :, :, :8] = 0
    return {"x": x.reshape(N, 128, 4 * C), "u": u.reshape(N, 128, 512), "v": d["v"], **weights(rng, w)}
def setup_inputs_near(rng):
    d = numbers_of(rng)
    x = np.zeros((N, 8, 16, C, 4), np.float32)
    u = d["u"].reshape(N, 128, 128, 4)
    u[:, :, ::16] = 0
    o, c = rng.permutation(N) % 4, signs(rng)
    upper = np.arange(C) // (C // 2)
    for r in range(N):
        i = (np.arange(C) + rng.integers(0, C, (8, 1))) % C
        if o[r] == 3: i = i % (C // 2) * 2 + upper
        s = (i + 1) // 2
        size = 1.0 if o[r] < 2 else 2.0 ** -4
        g = ((s[:, :, None] >> np.arange(8)) & 1) * np.exp2(np.arange(8) - 23.0) * size
        if o[r] < 2: x[r, :, 0, :, 0] = c[r][:, None]
        if o[r] == 3: x[r, :, 0, :, 0] = (8 + upper) * 2.0 ** -30
        x[r, :, 8] = g[:, :, :4]
        x[r, :, 9] = g[:, :, 4:]
        x[r, :, 10:] = rng.integers(4, 8, (8, 6, C, 4)) * 2.0 ** -20 * size
        k = 1.0 if o[r] == 0 else 2.0 ** -30
        for h in range(0, 128, 16):
            u[r, h, h, 0] = k
            u[r, h + 8:h + 10, h] = k
    w = layers(rng)
    w[:, :, :10] = 0
    w[:, :, :, :, :, :10] = 0
    return {"x": x.reshape(N, 128, 4 * C).astype(BF), "u": u.reshape(N, 128, 512), "v": d["v"], **weights(rng, w)}
def setup_inputs_huge(rng):
    d = numbers_of(rng)
    c = np.stack([rng.permutation(C) % 2 * 2.0 - 1.0 for r in range(N)])
    c[rng.permutation(N) < N // 2] = -1
    x = (0.6 + 0.2 * rng.random((N, 128, C, 4))) * np.where(c < 0, -2.0 ** 30, 2.0 ** 28)[:, None, :, None]
    u = d["u"].reshape(N, 128, 128, 4)
    a = 2.0 ** 30 * (1 - 0.25 * rng.random((N, 128, 8, 4))) * signs(rng)[:, None, :, None]
    u[:, :, ::16] = a.astype(np.float32).astype(BF)
    w = np.zeros((N, 128, 4, 128, 4), np.float32)
    i = np.arange(128)
    for b in range(4): w[:, i, b, i, b] = 16
    return {"x": x.astype(np.float32).reshape(N, 128, 4 * C).astype(BF), "u": u.reshape(N, 128, 512), "v": d["v"], **weights(rng, w.astype(BF))}
def setup_inputs_slots(rng):
    d = numbers_of(rng)
    s = np.zeros((N, 8, C), bool)
    h = int(rng.integers(8))
    for r in range(N):
        p = r ^ STEP[0]
        if r < p:
            n = rng.permutation(np.array([K, K - 1, K + 1, 2 * A, A, rng.integers(A, 2 * A + 1), rng.integers(A, 2 * A + 1)]))
            n = np.insert(n, h, A)
            for g in range(8):
                e = rng.permutation(C)
                s[r, g, e[:A]] = True
                s[p, g, e[n[g] - A:n[g]]] = True
    s[:, h] = np.isin(np.arange(C), rng.permutation(C)[:A])
    k = (s * rng.integers(8, 16, (N, 8, C)) * 0.125).astype(np.float32).astype(BF)
    x = d["x"].reshape(N, 8, 16, C, 4)
    x[:, :, :8] = 0
    u = d["u"].reshape(N, 128, 128, 4)
    u[:, :, ::16] = 0
    for r in range(N):
        x[:, :, r, :, 0] = k[r]
        for g in range(8): u[r, 16 * g + r, 16 * g, 0] = 1
    w = layers(rng)
    w[:, :, :, :, :, :8] = 0
    return {"x": x.reshape(N, 128, 4 * C), "u": u.reshape(N, 128, 512), "v": d["v"], **weights(rng, w)}
def setup_inputs_spread(rng):
    d = setup_inputs(rng)
    d["x"] = big(wide(rng, N, 128, 4 * C, cols=6))
    return d
def check_inputs(d):
    b = []
    for k in ("x", "u", "v"):
        a = np.abs(d[k].astype(np.float32))
        if not (np.isfinite(a).all() and ((a == 0) | (a >= 2.0 ** -30) & (a <= 2.0 ** 30)).all()): b.append("a value of " + k)
    none, least, most = [emit(mx_ref.quantize(np.full((128, 16), k, np.float32).astype(BF)))[1][0, 0] for k in (0.0, 2.0 ** -30, 2.0 ** 30)]
    for r in range(N):
        if ((d["wc"][r] == 0x7F) | (d["wc"][r] == 0xFF)).any(): b.append("wc: a code that is no number")
        s = mx_ref.live(d["ws"][r])
        if ((s != none) & ((s < least) | (s > most))).any(): b.append("ws: a scale out of range")
    return b
def reference(x, u, v, wc, ws):
    qu = [mx_ref.quantize(u[r]) for r in range(N)]
    lay = [pk(wc[r], ws[r]) for r in range(N)]
    now = [x[r] for r in range(N)]
    vec = np.zeros((N, 8, C, N), np.int64)
    for t in range(R):
        sent = []
        for r in range(N):
            e = order(mx_ref.matmul(qu[r], mx_ref.quantize(now[r])))[:, :A]
            z = gcols(now[r], e)
            q = mx_ref.quantize(z)
            h = tile([np.maximum(mx_ref.matmul(pick(lay[r], np.arange(128 * b, 128 * b + 128)), q), np.float32(0.0)) * np.float32(0.03125) + z[:, b::4].astype(np.float32) for b in range(4)])
            now[r] = gput(now[r], e, h)
            for g in range(8): vec[r, g, e[g], r] += 1
            sent.append(mx_ref.quantize(now[r]))
        came = decode(join(*sent)).astype(BF)
        had = vec.copy()
        for r in range(N):
            p = r ^ STEP[t]
            want = (had[p] > had[r]).any(axis=2)
            for g in range(8): want[g, np.flatnonzero(want[g])[K:]] = False
            newer = (had[p] >= had[r]).all(axis=2)
            c = cut(came, p, 4 * C)
            half = ((now[r].astype(np.float32) + c.astype(np.float32)) * np.float32(0.5)).astype(BF)
            new = now[r].copy()
            a, b = parts(want & newer), parts(want & ~newer)
            new[a] = c[a]
            new[b] = half[b]
            now[r] = new
            vec[r][want] = np.maximum(had[r], had[p])[want]
    y, ov = np.zeros((N, 128, C), np.float32), np.zeros((N, 8, C), np.float32)
    oc, osc = np.zeros((N, 128, 4 * C), np.uint8), np.zeros((N, 16, C), np.uint8)
    for r in range(N):
        q = mx_ref.quantize(now[r])
        y[r] = mx_ref.matmul(mx_ref.quantize(v[r]), q)
        ov[r] = np.sum(vec[r] * 4 ** np.arange(N), axis=2)
        oc[r], osc[r] = emit(q)
    return {"y": y, "ov": ov, "oc": oc, "osc": osc}

@@ -1,0 +1,509 @@
+from concourse.bass import DstId, RemoteDMATransfer
+from concourse.mybir import dt, AluOpType, ActivationFunctionType
+
+C, A, K, R = 352, 96, 160, 3
+STEP = [1, 6, 7]
+NK = C // 16
+KD = 13
+KS = KD - 1
+HALF = C // 2
+BIG = 2.0 ** 96
+LOW = 128.0
+SPAN = 4 * (A + C)
+HA = 128
+AH = HA + SPAN
+BH = AH + SPAN
+HB = BH + SPAN + 128
+WEND = HB + SPAN
+F8, U8, BF, F32, I32, U16 = "float8_e4m3fn_x4", "uint8", "bfloat16", "float32", "int32", "uint16"
+
+SCRATCH = {
+    "ps": ("psum", [128, 4096], F32),
+    "win": ("sbuf", [128, WEND], BF), "xh": ("sbuf", [128, 4 * C], BF), "oh": ("sbuf", [128, 4 * A], BF),
+    "zt": ("sbuf", [128, 512], BF), "rl": ("sbuf", [128, 4 * A], F32), "yt": ("sbuf", [128, C], F32),
+    "ut": ("sbuf", [128, 512], BF), "vt": ("sbuf", [128, 512], BF), "et": ("sbuf", [128, 2048], BF),
+    "qu": ("sbuf", [128, 128], F8), "su": ("sbuf", [128, 128], U8), "qur": ("sbuf", [128, 128], F8), "sur": ("sbuf", [128, 128], U8),
+    "qv": ("sbuf", [128, 128], F8), "sv": ("sbuf", [128, 128], U8), "qw": ("sbuf", [128, 512], F8), "sw": ("sbuf", [128, 512], U8),
+    "qe": ("sbuf", [128, 512], F8), "se": ("sbuf", [128, 512], U8), "qx": ("sbuf", [128, C], F8), "sx": ("sbuf", [128, C], U8),
+    "qz": ("sbuf", [128, 128], F8), "sz": ("sbuf", [128, 128], U8), "qh": ("sbuf", [128, 128], F8), "sh": ("sbuf", [128, 128], U8),
+    "pi": ("sbuf", [128, 4], I32), "pf": ("sbuf", [128, 2], F32), "k16": ("sbuf", [128, NK], F32), "uo": ("sbuf", [128, 8], U16),
+    "jt": ("sbuf", [128, C], F32), "md": ("sbuf", [128, C], F32), "rs": ("sbuf", [128, C], F32), "r01": ("sbuf", [128, C], BF),
+    "i4": ("sbuf", [128, C], F32), "c4": ("sbuf", [128, 48], F32), "cw2": ("sbuf", [128, NK], F32), "ck": ("sbuf", [128, NK], F32),
+    "tab": ("sbuf", [128, 256], F32),
+    "d1": ("sbuf", [128, C], F32), "fill": ("sbuf", [128, C], F32), "eq": ("sbuf", [128, C], BF), "nu": ("sbuf", [128, C], BF),
+    "fl": ("sbuf", [128, C * NK], BF), "sc": ("sbuf", [128, HALF * NK], BF), "gl": ("sbuf", [128, 3 * NK], F32),
+    "pl": ("sbuf", [128, NK], U16), "ew": ("sbuf", [128, C], F32), "eo": ("sbuf", [128, 24], U16), "so": ("sbuf", [128, 4 * NK], U16),
+    "cn": ("sbuf", [128, 96], BF), "df": ("sbuf", [128, 96], F32), "w": ("sbuf", [128, 24 * 26], F32), "wu": ("sbuf", [128, 64], U16),
+    "fo": ("sbuf", [128, 4 * NK], U16), "row": ("sbuf", [128, 3 * C], BF), "acc": ("sbuf", [128, 2], F32),
+    "pk": ("sbuf", [128, 192], F32), "ovr": ("sbuf", [128, C], F32),
+}
+for _t in range(R):
+    SCRATCH["lqh%d" % _t] = ("sbuf", [128, A + 128], F8)
+    SCRATCH["lsh%d" % _t] = ("sbuf", [128, A + 128], U8)
+    SCRATCH["lp%d" % _t] = ("sbuf", [128, NK], U16)
+    SCRATCH["le%d" % _t] = ("sbuf", [128, 6], U16)
+    if _t:
+        SCRATCH["lqx%d" % _t] = ("sbuf", [128, C], F8)
+        SCRATCH["lsx%d" % _t] = ("sbuf", [128, C], U8)
+        SCRATCH["lc%d" % _t] = ("sbuf", [128, 96], BF)
+SEMAPHORES = ["cv", "ca", "ct", "cg"] + ["a%s%d" % (k, t) for k in "hpexc" for t in range(R) if t or k in "hpe"] + ["d%d" % i for i in range(44)]
+
+
+def make_plan(g, T):
+    ops, free = [], ["d%d" % i for i in range(44)]
+
+    def view(name, a, b, step=1):
+        ap = T[name][:, a:b] if step == 1 else T[name][:, a:b:step]
+        if name == "ps":
+            a, b, step = a // 512 * 512, (b + 511) // 512 * 512, 1
+        return (ap, name, set(range(a, b, step)))
+
+    def note(q, fn, reads, writes, kind="c", sem=None, n=0):
+        if kind in "dr":
+            sem = free.pop(0)
+        ops.append({"q": q, "fn": fn, "r": reads, "w": writes, "kind": kind, "sem": sem, "n": n, "deps": [], "used": False})
+
+    def emit():
+        eng = {"v": g.vector, "a": g.scalar, "t": g.tensor, "g": g, "s": g.sync}
+        seen = {}
+        clock = {q: {} for q in eng}
+        for i, o in enumerate(ops):
+            need = set()
+            for (ap, name, cols), wr in [(x, False) for x in o["r"]] + [(x, True) for x in o["w"]]:
+                for j, c2, w2 in seen.get(name, []):
+                    if (wr or w2 or (name == "ps" and ops[j]["q"] != o["q"])) and not cols.isdisjoint(c2):
+                        need.add(j)
+            for (ap, name, cols), wr in [(x, False) for x in o["r"]] + [(x, True) for x in o["w"]]:
+                seen.setdefault(name, []).append((i, cols, wr))
+            if o["kind"] == "x":
+                o["clock"] = {o["sem"]: i}
+                continue
+            ck = clock[o["q"]]
+            for j in sorted(need, reverse=True):
+                key = ops[j]["sem"] or ops[j]["q"]
+                if ck.get(key, -1) < j:
+                    o["deps"].append(j)
+                    ops[j]["used"] = True
+                    for k2, v2 in ops[j]["clock"].items():
+                        ck[k2] = max(ck.get(k2, -1), v2)
+            o["clock"] = dict(ck)
+            o["clock"][o["sem"] or o["q"]] = i
+        count = {q: 0 for q in eng}
+        for o in ops:
+            e = eng.get(o["q"])
+            for j in o["deps"]:
+                e.wait_ge(T.sem[ops[j]["sem"] or "c" + ops[j]["q"]], ops[j]["n"])
+            if o["kind"] == "c":
+                ins = o["fn"](e)
+                if o["used"]:
+                    count[o["q"]] += 1
+                    o["n"] = count[o["q"]]
+                    ins.then_inc(T.sem["c" + o["q"]], 1)
+            elif o["kind"] == "d":
+                o["fn"](e).then_inc(T.sem[o["sem"]], 16)
+            elif o["kind"] == "r":
+                o["fn"](T.sem[o["sem"]])
+        for o in ops:
+            if o["kind"] != "c" and not o["used"]:
+                eng[o["q"]].wait_ge(T.sem[o["sem"]], o["n"])
+    return view, note, emit
+
+
+def rank_program(g, core, T, topo):
+    rank = T.rank_of(core)
+    if rank is None:
+        return
+    V, note, emit = make_plan(g, T)
+    Op, Fn = AluOpType, ActivationFunctionType
+
+    def ind(win, off):
+        return (win[0].indirect(off[0]), win[1], win[2], off)
+
+    def rd(*xs):
+        out = []
+        for x in xs:
+            if isinstance(x, tuple):
+                out.append(x[:3])
+                out.extend(x[3:])
+        return out
+
+    def ap(x):
+        return x[0] if isinstance(x, tuple) else x
+
+    def tt(out, a, b, op):
+        note("v", lambda e: e.tensor_tensor(out[0], a[0], b[0], op), rd(a, b), [out])
+
+    def ts(out, a, s1, op0, s2=None, op1=None):
+        if op1 is None:
+            note("v", lambda e: e.tensor_scalar(out[0], a[0], ap(s1), None, op0), rd(a, s1), [out])
+        else:
+            note("v", lambda e: e.tensor_scalar(out[0], a[0], ap(s1), ap(s2), op0, op1), rd(a, s1, s2), [out])
+
+    def cp(out, a):
+        note("v", lambda e: e.tensor_copy(out[0], a[0]), rd(a) + list(out[3:]), [out[:3]])
+
+    def scan(out, a, b, init, op0, op1):
+        note("v", lambda e: e.tensor_tensor_scan(out[0], a[0], b[0], ap(init), op0, op1), rd(a, b, init), [out])
+
+    def fillc(out, c):
+        note("v", lambda e: e.memset(out[0], c), [], [out])
+
+    def act(out, a, f, bias=None, scale=None, acc=None):
+        kw = {k: ap(x) for k, x in (("bias", bias), ("scale", scale), ("accum_out", acc)) if x is not None}
+        note("a", lambda e: e.activation(out[0], a[0], f, **kw), rd(a, bias), [out] + rd(acc))
+
+    def move(q, out, a):
+        if q == "v":
+            cp(out, a)
+        else:
+            act(out, a, Fn.Copy)
+
+    def quant(q, s, a):
+        note("v", lambda e: e.quantize_mx(q[0], s[0], a[0]), [a], [q, s])
+
+    def mm(bank, w, c0, x, a, n):
+        out, lq, lsc, rq, rsc = V("ps", 512 * bank, 512 * bank + n), V(w[0], c0, c0 + 128), V(w[1], c0, c0 + 128), V(x[0], a, a + n), V(x[1], a, a + n)
+        note("t", lambda e: e.matmul_mx(out[0], lq[0], lsc[0], rq[0], rsc[0], True, True), [lq, lsc, rq, rsc], [out])
+
+    def iota(out, pattern, base, cm, small=True):
+        if small:
+            note("g", lambda e: e.iota(out[0], pattern, base, cm, allow_small_or_imprecise_dtypes=True), [], [out])
+        else:
+            note("g", lambda e: e.iota(out[0], pattern, base, cm), [], [out])
+
+    def dma(q, out, in_, reads, writes):
+        note(q, lambda e: e.dma_start(out, in_), reads, writes, kind="d", n=16)
+
+    def u8(x):
+        return x[0].bitcast(dt.uint8) if SCRATCH[x[1]][2] == F8 else x[0]
+
+    def send(t, sem, pairs):
+        to = T.cores[rank ^ STEP[t]]
+        rid, pid = topo.addr(to, core)
+        en = topo.engines(core, to)
+        if len(pairs) == 1:
+            src, dst = pairs[0]
+            note("g", lambda ls: g.remote_dma(u8(dst), u8(src), T.sem[sem], ls, pid, rid, topo.mask(core, to)), [src], [], kind="r", n=len(en))
+        else:
+            m = len(en) // len(pairs)
+            trs = [RemoteDMATransfer(dst_ids=[DstId(rid=rid, pnc=pid)], dma_engine_mask=sum(1 << e for e in en[m * i:m * i + m]),
+                                     remote_sem=T.sem[sem], src=u8(s), dst=u8(d)) for i, (s, d) in enumerate(pairs)]
+            note("g", lambda ls: g.remote_dma_fused(trs, local_sem=ls), [s for s, d in pairs], [], kind="r", n=m * len(pairs))
+
+    def landed(t, sem, calls, views):
+        note("x", None, [], views, kind="x", sem=sem, n=calls * len(topo.engines(T.cores[rank ^ STEP[t]], core)))
+
+    def W(i, n=NK):
+        return V("w", 24 * i, 24 * i + n)
+
+    def slot(out, places, i, base):
+        return [lambda: ts(W(i), places, 4.0, Op.mult, float(base), Op.add),
+                lambda: ts(W(i + 1), places, A - 0.5, Op.subtract, 16384.0, Op.mult),
+                lambda: tt(W(i), W(i), W(i + 1), Op.max),
+                lambda: tt(out, W(i), V("c4", 24, 24 + NK) if base else V("c4", 0, NK), Op.min)]
+
+    def digit(i, src, f):
+        at = 48 * i + (24 if f == Fn.Relu else 0)
+        act(V("pk", at, at + 24), V(src, 24 * i, 24 * i + 24), f, scale=4.0 ** i)
+
+    XA = HA + 4 * A
+    dma("s", T.ut[:], T.u[:], [], [V("ut", 0, 512)])
+    dma("a", T.win[:, XA:XA + 2 * C], T.x[:, 0:2 * C], [], [V("win", XA, XA + 2 * C)])
+    dma("s", T.win[:, XA + 2 * C:XA + 4 * C], T.x[:, 2 * C:4 * C], [], [V("win", XA + 2 * C, XA + 4 * C)])
+    later = [V("win", XA, XA + 4 * C)]
+    dma("s", T.qw[:].bitcast(dt.uint8), T.wc[:], later, [V("qw", 0, 512)])
+    dma("s", T.sw[:], T.ws[:], [], [V("sw", 0, 512)])
+    dma("s", T.vt[:], T.v[:], [], [V("vt", 0, 512)])
+    fillc(V("et", 0, 2048), 0.0)
+    iota(V("pi", 0, 2), [[0, 2]], 0, 1, small=False)
+    iota(V("k16", 0, NK), [[16, NK]], 0, 0)
+    iota(V("jt", 0, C), [[0, NK], [1, 16]], 0, 0)
+    iota(V("i4", 0, C), [[4, C]], 0, 0)
+    et = V("et", 0, 2048)
+    note("g", lambda e: e.affine_select(et[0], et[0], [[-1, 4], [1, 512]], Op.not_equal, 0.5, 0, -4), [et], [et])
+    rel = [rank, rank ^ STEP[0], rank ^ STEP[2], rank ^ STEP[1]]
+    for d3 in range(4):
+        iota(V("tab", 64 * d3, 64 * d3 + 64), [[4 ** rel[2], 4], [4 ** rel[1], 4], [4 ** rel[0], 4]], d3 * 4 ** rel[3], 0)
+    cp(V("uo", 0, 8), V("k16", 0, 8))
+    ts(V("pi", 2, 4), V("pi", 0, 2), 15, Op.bitwise_and)
+    fillc(V("win", 0, HA), 0.0)
+    cp(V("pf", 0, 2), V("pi", 2, 4))
+    qcol = V("pf", 0, 1)
+    fillc(V("win", HB - 128, HB), 0.0)
+    ts(V("md", 0, C), V("jt", 0, C), qcol, Op.is_equal, 2 * BIG, Op.mult)
+    fillc(V("zt", 0, 128), 0.0)
+    fillc(V("cn", 0, 96), 0.0)
+    fillc(V("gl", 2 * NK - 1, 2 * NK), 0.0)
+    fillc(V("ck", 0, KD), -LOW)
+    ts(V("c4", 0, NK), V("k16", 0, NK), qcol, Op.add, 4.0, Op.mult)
+    ts(V("ck", KD, NK), V("k16", KD, NK), 16.0 - LOW, Op.add)
+    ts(V("cw2", 0, NK), V("c4", 0, NK), 0.5, Op.mult, -1.0 * C, Op.add)
+    ts(V("c4", 24, 24 + NK), V("c4", 0, NK), 4.0 * A + SPAN, Op.add)
+    ts(V("c4", 0, NK), V("c4", 0, NK), 4.0 * A, Op.add)
+    act(V("r01", 0, C), V("jt", 0, C), Fn.Sign)
+    act(V("rs", 0, C), V("r01", 0, C), Fn.Identity, bias=-BIG, scale=2 * BIG)
+    act(V("md", 0, C), V("md", 0, C), Fn.Identity, bias=-BIG)
+    quant(V("qu", 0, 128), V("su", 0, 128), V("ut", 0, 512))
+    uo = V("uo", 0, 8)
+    note("v", lambda e: e.tensor_copy(T.qur[:, 0:128].bitcast(dt.uint32), T.qu[:, 0:128].bitcast(dt.uint32).indirect(uo[0])), [V("qu", 0, 128), uo], [V("qur", 0, 128)])
+    act(V("sur", 0, 128), ind(V("su", 0, 128), uo), Fn.Copy)
+
+    QX, QE = ("qx", "sx"), ("qe", "se")
+    wr, spS, wp, spp, old, recv, t2, t3, t4, t5, some, sp, pw = [W(i) for i in range(13)]
+    for t in range(R):
+        H0, H1 = (HA, HB) if t % 2 == 0 else (HB, HA)
+        X0, X1 = H0 + 4 * A, H1 + 4 * A
+        small = V("win", H0, H0 + SPAN)
+        lo, hi = (HA, BH + (4 * A if t == 0 else SPAN)) if t % 2 == 0 else (AH, WEND)
+        if t == 0:
+            for a in (0, HALF):
+                quant(V("qx", a, a + HALF), V("sx", a, a + HALF), V("win", X0 + 4 * a, X0 + 4 * a + 2 * C))
+        else:
+            quant(V("qx", 0, C), V("sx", 0, C), V("win", X0, X0 + 4 * C))
+        mm(0, ("qur", "sur"), 0, QX, 0, C)
+        mm(1, ("qur", "sur"), 0, QX, 0, C)
+        if t == 1:
+            cp(V("cn", 24, 24 + NK), recv)
+        if t == 2:
+            tt(V("cn", 72, 72 + NK), pw, recv, Op.mult)
+            tt(V("cn", 48, 48 + NK), V("lc1", 48, 48 + NK), recv, Op.mult)
+            for i in range(1, 4):
+                digit(i, "cn", Fn.Copy)
+        if t:
+            lqx, lsx, lc = "lqx%d" % t, "lsx%d" % t, "lc%d" % t
+            send(t, "ax%d" % t, [(V("qx", 0, C), V(lqx, 0, C))])
+            send(t, "ax%d" % t, [(V("sx", 0, C), V(lsx, 0, C))])
+            if t == 1:
+                send(t, "ac1", [(V("cn", 0, NK), V(lc, 72, 72 + NK)), (V("cn", 24, 24 + NK), V(lc, 48, 48 + NK))])
+            else:
+                send(t, "ac2", [(V("cn", 0, 48), V(lc, 48, 96)), (V("cn", 48, 96), V(lc, 0, 48))])
+            landed(t, "ax%d" % t, 2, [V(lqx, 0, C), V(lsx, 0, C)])
+            landed(t, "ac%d" % t, 1, [V(lc, 0, 96)])
+            for b in range(4):
+                mm(4 + b, QE, 128 * b, (lqx, lsx), 0, C)
+        for a, b in ((16 * KS, C), (0, 16 * KS)):
+            tt(V("d1", a, b), V("ps", a, b), V("md", a, b), Op.min)
+            scan(V("fill", a, b), V("rs", a, b), V("d1", a, b), -BIG, Op.min, Op.max)
+        tt(V("eq", 0, C), V("ps", 0, C), V("fill", 0, C), Op.is_equal)
+
+        def own(k):
+            return V("fill", 16 * k + 15, 16 * k + 16)
+
+        def vec_cmp(k):
+            e = 16 * k + 16
+            ts(V("fl", C * k, C * k + e), V("ps", 0, e), own(k), Op.is_ge)
+            if k < KS:
+                ts(V("fl", C * k + e, C * k + C), V("ps", e, C), own(k), Op.is_gt)
+
+        def vec_sum(k):
+            h = HALF if k < KS else 8 * k + 8
+            scan(V("sc", HALF * (k + 1) - h, HALF * (k + 1)), V("fl", C * k, C * k + h), V("fl", C * k + h, C * k + 2 * h),
+                 V("gl", 2 * NK + k, 2 * NK + k + 1), Op.add, Op.add)
+
+        def act_cmp(k):
+            a = 0 if k > KS else 16 * k + 16
+            act(V("fl", C * k + a, C * k + C), V("ps", 512 + a, 512 + C), Fn.Sign, bias=own(k), scale=-1.0)
+
+        def act_less(k):
+            x = V("fl", C * k, C * k + 16 * k + 16)
+            act(x, x, Fn.Relu, acc=V("gl", k, k + 1))
+
+        def act_more(k):
+            if k + 1 < NK:
+                x = V("fl", C * k + 16 * k + 16, C * k + C)
+                act(x, x, Fn.Relu, scale=-1.0, acc=V("gl", NK + k, NK + k + 1))
+        vec_cmp(0)
+        scan(V("nu", 0, C), V("r01", 0, C), V("eq", 0, C), 0.0, Op.mult, Op.subtract)
+        vec_cmp(1)
+        tt(V("gl", 2 * NK, 3 * NK), V("nu", 15, C, 16), V("ck", 0, NK), Op.add)
+        for k in range(2, KD):
+            vec_cmp(k)
+            vec_sum(k - 2)
+        vec_sum(KD - 2)
+        vec_sum(KD - 1)
+        act_cmp(NK - 1)
+        for k in range(NK - 2, KD - 1, -1):
+            act_cmp(k)
+            act_less(k + 1)
+            if k > KD:
+                act_more(k + 1)
+        act_cmp(KS)
+        act_less(KD)
+        for k in (KD + 1, KD, KS):
+            act_more(k)
+        if t:
+            for b in range(4):
+                act(V("win", AH + 4 * A + b, BH, 4), V("ps", 512 * (4 + b), 512 * (4 + b) + C), Fn.Copy, scale=2.0)
+        tt(V("sc", HALF * KD + HALF - 1, HALF * NK, HALF), V("gl", 2 * NK + KD, 3 * NK), V("gl", KD, NK), Op.subtract)
+        x = V("sc", HALF * KS + HALF - 1, HALF * NK, HALF)
+        tt(x, x, V("gl", NK + KS, 2 * NK), Op.add)
+        pl, lp, le = V("pl", 0, NK), V("lp%d" % t, 0, NK), V("le%d" % t, 0, 6)
+        ts(pl, V("sc", HALF - 1, HALF * NK, HALF), LOW, Op.add)
+        send(t, "ap%d" % t, [(pl, lp)])
+        landed(t, "ap%d" % t, 1, [lp])
+        cp(ind(V("ew", 0, C), pl), V("i4", 0, C))
+        tt(V("d1", 0, A), V("ew", 0, A), V("md", 0, A), Op.min)
+        scan(V("fill", 0, A), V("rs", 0, A), V("d1", 0, A), -BIG, Op.min, Op.max)
+        for b in (1, 2, 3, 0):
+            ts(V("eo", 6 * b, 6 * b + 6), V("fill", 15, A, 16), float(b), Op.add)
+        for b in (1, 2, 3, 0):
+            move("a" if b else "v", V("zt", 128 + b, 512, 4), ind(V("win", X0, X0 + 4 * C), V("eo", 6 * b, 6 * b + 6)))
+        send(t, "ae%d" % t, [(V("eo", 0, 6), le)])
+        landed(t, "ae%d" % t, 1, [le])
+        mine, theirs = slot(sp, pl, 13, 0), slot(spp, lp, 15, AH - lo)
+        mine[0]()
+        mine[1]()
+        quant(V("qz", 0, 128), V("sz", 0, 128), V("zt", 0, 512))
+        for b in range(4):
+            mm(b, ("qw", "sw"), 128 * b, ("qz", "sz"), 0, 128)
+
+        def spo(b, make=False):
+            if make:
+                ts(spo(b), sp, float(b), Op.add)
+            return V("so", NK * b, NK * b + NK)
+        mine[2]()
+        ts(wr, pl, float(A), Op.is_lt)
+        mine[3]()
+        tt(V("cn", 0, NK), V("cn", 0, NK), wr, Op.add)
+        spo(0, True)
+        for b in range(4):
+            act(V("rl", A * b, A * b + A), V("ps", 512 * b + 32, 512 * b + 128), Fn.Relu, scale=0.03125)
+            tt(V("win", H0 + b, X0, 4), V("rl", A * b, A * b + A), V("zt", 128 + b, 512, 4), Op.add)
+        quant(V("qh", 0, 128), V("sh", 0, 128), V("win", H0 - 128, X0))
+        lqh, lsh = "lqh%d" % t, "lsh%d" % t
+        send(t, "ah%d" % t, [(V("qh", 32, 128), V(lqh, 0, A))])
+        send(t, "ah%d" % t, [(V("sh", 32, 128), V(lsh, 0, A))])
+
+        def half(b, q):
+            if q == "v":
+                ts(V("xh", C * b, C * b + C), ind(small, spo(b)), 0.5, Op.mult)
+            else:
+                act(V("xh", C * b, C * b + C), ind(small, spo(b)), Fn.Copy, scale=0.5)
+
+        def mean(b):
+            tt(V("win", BH + 4 * A + b, BH + SPAN, 4), V("ps", 512 * (4 + b), 512 * (4 + b) + C), V("xh", C * b, C * b + C), Op.add)
+
+        def owns(b):
+            act(V("oh", A * b, A * b + A), ind(V("xh", C * b, C * b + C), ep), Fn.Copy)
+        ep, wantu = V("wu", 0, 6), V("wu", 8, 8 + NK)
+        if t == 2:
+            digit(0, "cn", Fn.Copy)
+        half(0, "a")
+        spo(1, True)
+        half(1, "a")
+        if t == 0:
+            spo(2, True)
+            spo(3, True)
+            half(2, "v")
+            half(3, "a")
+            fillc(V("win", AH + 4 * A, BH), 0.0)
+            quant(V("qe", 0, 512), V("se", 0, 512), et)
+            theirs[0]()
+            theirs[1]()
+            ts(ep, le, 0.25, Op.mult)
+            for i in range(R):
+                quant(V("lqh%d" % i, A, A + 128), V("lsh%d" % i, A, A + 128), V("win", AH + 4 * A, AH + 4 * A + 512))
+            theirs[2]()
+            ts(old, wr, float(SPAN), Op.mult)
+            theirs[3]()
+            ts(recv, lp, float(A), Op.is_lt)
+            for b in range(4):
+                owns(b)
+            tt(t2, spp, old, Op.add)
+            fillc(V("pk", 24, 48), 0.0)
+            tt(t3, t2, sp, Op.subtract)
+        else:
+            ts(wp, lp, float(A), Op.is_lt)
+            if t == 1:
+                spo(2, True)
+                tt(pw, V(lc, 72, 72 + NK), wp, Op.add)
+                spo(3, True)
+                tt(some, pw, V(lc, 48, 48 + NK), Op.add)
+            else:
+                tt(V("df", 0, 96), V(lc, 0, 96), V("cn", 0, 96), Op.subtract)
+                spo(2, True)
+                tt(W(17), V("df", 24, 24 + NK), V("df", 72, 72 + NK), Op.max)
+                tt(V("df", 48, 48 + NK), V("df", 48, 48 + NK), wp, Op.add)
+                spo(3, True)
+                tt(some, W(17), V("df", 48, 48 + NK), Op.max)
+            theirs[0]()
+            ts(wantu, some, 0.0, Op.is_gt)
+            act(V("row", 0, C), ind(V("i4", 0, 16), wantu), Fn.Copy)
+            theirs[1]()
+            mean(0)
+            theirs[2]()
+            if t == 1:
+                tt(W(18), V("cn", 0, NK), V("cn", 24, 24 + NK), Op.add)
+            else:
+                tt(W(18, 48), V("df", 0, 48), V("df", 48, 96), Op.min)
+            theirs[3]()
+            scan(V("row", C, 2 * C), V("row", 0, C), V("row", 0, C), 0.0, Op.add, Op.max)
+            half(2, "a")
+            act(V("row", 2 * C, 3 * C), V("row", C, 2 * C), Fn.Sign, bias=4.0 * K + 2.0, scale=-1.0, acc=V("acc", 0, 1))
+            half(3, "a")
+            if t == 1:
+                ts(spS, sp, float(H0 - lo), Op.add)
+                ts(some, some, 0.0, Op.is_gt)
+                ts(old, W(18), 0.0, Op.is_gt, float(SPAN), Op.mult)
+            else:
+                tt(W(18), W(18), W(19), Op.min)
+                ts(some, some, 0.0, Op.is_gt)
+                ts(old, W(18), 0.0, Op.is_lt, float(SPAN), Op.mult)
+            mean(1)
+            tt(t2, spp, old, Op.add)
+            ts(ep, le, 0.25, Op.mult)
+            tt(t3, t2, spS if t == 1 else sp, Op.subtract)
+            for b in range(4):
+                owns(b)
+            ts(W(17), V("cw2", 0, NK), V("acc", 0, 1), Op.is_lt)
+            tt(t3, t3, some, Op.mult)
+            mean(2)
+        tt(t4, t3, recv if t == 0 else W(17), Op.mult)
+        if t:
+            tt(recv, W(17), some, Op.mult)
+        else:
+            quant(V("qv", 0, 128), V("sv", 0, 128), V("vt", 0, 512))
+        tt(t5, t4, spS if t == 1 else sp, Op.add)
+        if t:
+            mean(3)
+        for b in range(4):
+            ts(V("fo", NK * b, NK * b + NK), t5, float(b), Op.add)
+        steps = []
+        if t == 2:
+            for i in range(1, 4):
+                digit(i, "df", Fn.Relu)
+            steps = [lambda: tt(W(20, 96), V("pk", 0, 96), V("pk", 96, 192), Op.add),
+                     lambda: tt(W(20, 48), W(20, 48), W(22, 48), Op.add),
+                     lambda: tt(W(21), W(21), recv, Op.mult),
+                     lambda: tt(W(20), W(20), W(21), Op.add)]
+        landed(t, "ah%d" % t, 2, [V(lqh, 0, A), V(lsh, 0, A)])
+        for b in range(4):
+            mm(b, QE, 128 * b, (lqh, lsh), 0, 128)
+        for b in range(4):
+            tt(V("win", BH + b, BH + 4 * A, 4), V("ps", 512 * b, 512 * b + A), V("oh", A * b, A * b + A), Op.add)
+            act(V("win", AH + b, AH + 4 * A, 4), V("ps", 512 * b, 512 * b + A), Fn.Copy, scale=2.0)
+        if steps:
+            steps[0]()
+            steps[1]()
+        if t + 1 < R:
+            for b in range(4):
+                move("v" if b < 2 else "a", V("win", X1 + b, X1 + 4 * C, 4), ind(V("win", lo, hi), V("fo", NK * b, NK * b + NK)))
+    runs = ((0, 12), (12, NK))
+    for i, (k0, k1) in enumerate(runs):
+        a, z = 16 * k0, 16 * k1
+        for b in range(4):
+            move("v" if b < 2 else "a", V("win", X1 + 4 * a + b, X1 + 4 * z, 4), ind(V("win", lo, hi), V("fo", NK * b + k0, NK * b + k1)))
+        steps[2 + i]()
+        quant(V("qx", a, z), V("sx", a, z), V("win", X1 + 4 * a, X1 + 4 * z))
+        mm(i, ("qv", "sv"), 0, QX, a, z - a)
+        dma("s", T.oc[:, 4 * a:4 * z], T.qx[:, a:z].bitcast(dt.uint8), [V("qx", a, z)], [])
+    cp(V("wu", 32, 32 + NK), W(20))
+    cp(V("ovr", 0, C), ind(V("tab", 0, 256), V("wu", 32, 32 + NK)))
+    for i, (k0, k1) in enumerate(runs):
+        a, z = 16 * k0, 16 * k1
+        act(V("yt", a, z), V("ps", 512 * i, 512 * i + z - a), Fn.Copy)
+        dma("a", T.y[:, a:z], T.yt[:, a:z], [V("yt", a, z)], [])
+    for k in range(4):
+        dma("s", T.osc[4 * k:4 * k + 4, :], T.sx[32 * k:32 * k + 4, :], [V("sx", 0, C)], [])
+    dma("s", T.ov[:], T.ovr[0:128:16, :], [V("ovr", 0, C)], [])
+    emit()

@@ -4,49 +4,46 @@ from concourse.mybir import dt, AluOpType, ActivationFunctionType
 C, A, K, R = 352, 96, 160, 3
 STEP = [1, 6, 7]
 NK = C // 16
-KD = 13
-KS = KD - 1
+NL, NH = 5, 16
 HALF = C // 2
+ROW = C + 2
 BIG = 2.0 ** 96
 LOW = 128.0
-SPAN = 4 * (A + C)
-HA = 128
-AH = HA + SPAN
-BH = AH + SPAN
-HB = BH + SPAN + 128
-WEND = HB + SPAN
+PAIR = C + A
+OFF = 2 * PAIR
+ONE = 4096.0
+JUMP = 65536.0
 F8, U8, BF, F32, I32, U16 = "float8_e4m3fn_x4", "uint8", "bfloat16", "float32", "int32", "uint16"
 
 SCRATCH = {
     "ps": ("psum", [128, 4096], F32),
-    "win": ("sbuf", [128, WEND], BF), "xh": ("sbuf", [128, 4 * C], BF), "oh": ("sbuf", [128, 4 * A], BF),
-    "zt": ("sbuf", [128, 512], BF), "rl": ("sbuf", [128, 4 * A], F32), "yt": ("sbuf", [128, C], F32),
+    "w0": ("sbuf", [128, 4 * (PAIR + 2 * A)], BF), "w1": ("sbuf", [128, 12 * PAIR], BF), "w2": ("sbuf", [128, 12 * PAIR], BF),
+    "w3": ("sbuf", [128, 4 * C], BF), "xh": ("sbuf", [128, 4 * C], BF), "oh": ("sbuf", [128, 4 * A], BF),
+    "zt": ("sbuf", [128, 512], BF), "rl": ("sbuf", [128, 4 * A], F32), "yt": ("sbuf", [128, C], F32), "nil": ("sbuf", [128, 512], BF),
     "ut": ("sbuf", [128, 512], BF), "vt": ("sbuf", [128, 512], BF), "et": ("sbuf", [128, 2048], BF),
     "qu": ("sbuf", [128, 128], F8), "su": ("sbuf", [128, 128], U8), "qur": ("sbuf", [128, 128], F8), "sur": ("sbuf", [128, 128], U8),
     "qv": ("sbuf", [128, 128], F8), "sv": ("sbuf", [128, 128], U8), "qw": ("sbuf", [128, 512], F8), "sw": ("sbuf", [128, 512], U8),
     "qe": ("sbuf", [128, 512], F8), "se": ("sbuf", [128, 512], U8), "qx": ("sbuf", [128, C], F8), "sx": ("sbuf", [128, C], U8),
     "qz": ("sbuf", [128, 128], F8), "sz": ("sbuf", [128, 128], U8), "qh": ("sbuf", [128, 128], F8), "sh": ("sbuf", [128, 128], U8),
-    "pi": ("sbuf", [128, 4], I32), "pf": ("sbuf", [128, 2], F32), "k16": ("sbuf", [128, NK], F32), "uo": ("sbuf", [128, 8], U16),
+    "pi": ("sbuf", [128, 8], I32), "pf": ("sbuf", [128, 8], F32), "k16": ("sbuf", [128, NK], F32), "uo": ("sbuf", [128, 8], U16),
     "jt": ("sbuf", [128, C], F32), "md": ("sbuf", [128, C], F32), "rs": ("sbuf", [128, C], F32), "r01": ("sbuf", [128, C], BF),
-    "i4": ("sbuf", [128, C], F32), "c4": ("sbuf", [128, 48], F32), "cw2": ("sbuf", [128, NK], F32), "ck": ("sbuf", [128, NK], F32),
-    "tab": ("sbuf", [128, 256], F32),
+    "i4": ("sbuf", [128, C], F32), "j4": ("sbuf", [128, A], F32), "hold": ("sbuf", [128, 4 * A], F32), "col": ("sbuf", [128, 72], F32),
+    "tab": ("sbuf", [128, 256], F32), "any": ("sbuf", [128, 3 * PAIR], BF),
     "d1": ("sbuf", [128, C], F32), "fill": ("sbuf", [128, C], F32), "eq": ("sbuf", [128, C], BF), "nu": ("sbuf", [128, C], BF),
-    "fl": ("sbuf", [128, C * NK], BF), "sc": ("sbuf", [128, HALF * NK], BF), "gl": ("sbuf", [128, 3 * NK], F32),
-    "pl": ("sbuf", [128, NK], U16), "ew": ("sbuf", [128, C], F32), "eo": ("sbuf", [128, 24], U16), "so": ("sbuf", [128, 4 * NK], U16),
-    "cn": ("sbuf", [128, 96], BF), "df": ("sbuf", [128, 96], F32), "w": ("sbuf", [128, 24 * 26], F32), "wu": ("sbuf", [128, 64], U16),
+    "fl": ("sbuf", [128, ROW * NK], BF), "sc": ("sbuf", [128, HALF * NK], BF), "gl": ("sbuf", [128, NK], F32),
+    "pl": ("sbuf", [128, NK], U16), "ew": ("sbuf", [128, C], F32), "eh": ("sbuf", [128, 2 * A], F32), "zl": ("sbuf", [128, 24], U16),
+    "ml": ("sbuf", [128, 28], U16), "so": ("sbuf", [128, 4 * NK], U16),
+    "cn": ("sbuf", [128, 96], BF), "df": ("sbuf", [128, 96], F32), "w": ("sbuf", [128, 24 * 20], F32), "wu": ("sbuf", [128, NK], U16),
     "fo": ("sbuf", [128, 4 * NK], U16), "row": ("sbuf", [128, 3 * C], BF), "acc": ("sbuf", [128, 2], F32),
     "pk": ("sbuf", [128, 192], F32), "ovr": ("sbuf", [128, C], F32),
 }
 for _t in range(R):
-    SCRATCH["lqh%d" % _t] = ("sbuf", [128, A + 128], F8)
-    SCRATCH["lsh%d" % _t] = ("sbuf", [128, A + 128], U8)
-    SCRATCH["lp%d" % _t] = ("sbuf", [128, NK], U16)
-    SCRATCH["le%d" % _t] = ("sbuf", [128, 6], U16)
+    SCRATCH["lq%d" % _t] = ("sbuf", [128, (C if _t else 128) + A], F8)
+    SCRATCH["ls%d" % _t] = ("sbuf", [128, (C if _t else 128) + A], U8)
+    SCRATCH["lm%d" % _t] = ("sbuf", [128, 28], U16)
     if _t:
-        SCRATCH["lqx%d" % _t] = ("sbuf", [128, C], F8)
-        SCRATCH["lsx%d" % _t] = ("sbuf", [128, C], U8)
-        SCRATCH["lc%d" % _t] = ("sbuf", [128, 96], BF)
-SEMAPHORES = ["cv", "ca", "ct", "cg"] + ["a%s%d" % (k, t) for k in "hpexc" for t in range(R) if t or k in "hpe"] + ["d%d" % i for i in range(44)]
+        SCRATCH["lc%d" % _t] = ("sbuf", [128, 48 * _t], BF)
+SEMAPHORES = ["cv", "ca", "ct", "cg"] + ["a%s%d" % (k, t) for k in "hmxc" for t in range(R) if t or k in "hm"] + ["d%d" % i for i in range(44)]
 
 
 def make_plan(g, T):
@@ -105,7 +102,7 @@ def make_plan(g, T):
                 o["fn"](T.sem[o["sem"]])
         for o in ops:
             if o["kind"] != "c" and not o["used"]:
-                eng[o["q"]].wait_ge(T.sem[o["sem"]], o["n"])
+                eng[o["q"] if o["q"] in eng else "g"].wait_ge(T.sem[o["sem"]], o["n"])
     return view, note, emit
 
 
@@ -152,11 +149,13 @@ def rank_program(g, core, T, topo):
         kw = {k: ap(x) for k, x in (("bias", bias), ("scale", scale), ("accum_out", acc)) if x is not None}
         note("a", lambda e: e.activation(out[0], a[0], f, **kw), rd(a, bias), [out] + rd(acc))
 
-    def move(q, out, a):
-        if q == "v":
+    def move(q, out, a, scale=None):
+        if q == "a":
+            act(out, a, Fn.Copy, scale=scale)
+        elif scale is None:
             cp(out, a)
         else:
-            act(out, a, Fn.Copy)
+            ts(out, a, scale, Op.mult)
 
     def quant(q, s, a):
         note("v", lambda e: e.quantize_mx(q[0], s[0], a[0]), [a], [q, s])
@@ -177,18 +176,10 @@ def rank_program(g, core, T, topo):
     def u8(x):
         return x[0].bitcast(dt.uint8) if SCRATCH[x[1]][2] == F8 else x[0]
 
-    def send(t, sem, pairs):
+    def send(t, sem, src, dst):
         to = T.cores[rank ^ STEP[t]]
         rid, pid = topo.addr(to, core)
-        en = topo.engines(core, to)
-        if len(pairs) == 1:
-            src, dst = pairs[0]
-            note("g", lambda ls: g.remote_dma(u8(dst), u8(src), T.sem[sem], ls, pid, rid, topo.mask(core, to)), [src], [], kind="r", n=len(en))
-        else:
-            m = len(en) // len(pairs)
-            trs = [RemoteDMATransfer(dst_ids=[DstId(rid=rid, pnc=pid)], dma_engine_mask=sum(1 << e for e in en[m * i:m * i + m]),
-                                     remote_sem=T.sem[sem], src=u8(s), dst=u8(d)) for i, (s, d) in enumerate(pairs)]
-            note("g", lambda ls: g.remote_dma_fused(trs, local_sem=ls), [s for s, d in pairs], [], kind="r", n=m * len(pairs))
+        note("g", lambda ls: g.remote_dma(u8(dst), u8(src), T.sem[sem], ls, pid, rid, topo.mask(core, to)), [src], [], kind="r", n=len(topo.engines(core, to)))
 
     def landed(t, sem, calls, views):
         note("x", None, [], views, kind="x", sem=sem, n=calls * len(topo.engines(T.cores[rank ^ STEP[t]], core)))
@@ -196,21 +187,17 @@ def rank_program(g, core, T, topo):
     def W(i, n=NK):
         return V("w", 24 * i, 24 * i + n)
 
-    def slot(out, places, i, base):
-        return [lambda: ts(W(i), places, 4.0, Op.mult, float(base), Op.add),
-                lambda: ts(W(i + 1), places, A - 0.5, Op.subtract, 16384.0, Op.mult),
-                lambda: tt(W(i), W(i), W(i + 1), Op.max),
-                lambda: tt(out, W(i), V("c4", 24, 24 + NK) if base else V("c4", 0, NK), Op.min)]
+    def cn(i, n=NK):
+        return V("cn", 24 * i, 24 * i + n)
 
     def digit(i, src, f):
         at = 48 * i + (24 if f == Fn.Relu else 0)
-        act(V("pk", at, at + 24), V(src, 24 * i, 24 * i + 24), f, scale=4.0 ** i)
+        act(V("pk", at, at + 24), V(src, 24 * i, 24 * i + 24), f, scale=(-1.0 if f == Fn.Relu else 1.0) * 4.0 ** i / ONE)
 
-    XA = HA + 4 * A
     dma("s", T.ut[:], T.u[:], [], [V("ut", 0, 512)])
-    dma("a", T.win[:, XA:XA + 2 * C], T.x[:, 0:2 * C], [], [V("win", XA, XA + 2 * C)])
-    dma("s", T.win[:, XA + 2 * C:XA + 4 * C], T.x[:, 2 * C:4 * C], [], [V("win", XA + 2 * C, XA + 4 * C)])
-    later = [V("win", XA, XA + 4 * C)]
+    dma("a", T.w0[:, 0:2 * C], T.x[:, 0:2 * C], [], [V("w0", 0, 2 * C)])
+    dma("s", T.w0[:, 2 * C:4 * C], T.x[:, 2 * C:4 * C], [], [V("w0", 2 * C, 4 * C)])
+    later = [V("w0", 0, 4 * C)]
     dma("s", T.qw[:].bitcast(dt.uint8), T.wc[:], later, [V("qw", 0, 512)])
     dma("s", T.sw[:], T.ws[:], [], [V("sw", 0, 512)])
     dma("s", T.vt[:], T.v[:], [], [V("vt", 0, 512)])
@@ -218,292 +205,316 @@ def rank_program(g, core, T, topo):
     iota(V("pi", 0, 2), [[0, 2]], 0, 1, small=False)
     iota(V("k16", 0, NK), [[16, NK]], 0, 0)
     iota(V("jt", 0, C), [[0, NK], [1, 16]], 0, 0)
+    iota(V("j4", 0, A), [[0, A // 4], [1, 4]], 0, 0)
     iota(V("i4", 0, C), [[4, C]], 0, 0)
     et = V("et", 0, 2048)
     note("g", lambda e: e.affine_select(et[0], et[0], [[-1, 4], [1, 512]], Op.not_equal, 0.5, 0, -4), [et], [et])
-    rel = [rank, rank ^ STEP[0], rank ^ STEP[2], rank ^ STEP[1]]
-    for d3 in range(4):
-        iota(V("tab", 64 * d3, 64 * d3 + 64), [[4 ** rel[2], 4], [4 ** rel[1], 4], [4 ** rel[0], 4]], d3 * 4 ** rel[3], 0)
+    q16, q4, b4, back16, back4 = [V("pf", i, i + 1) for i in (0, 2, 4, 6, 7)]
+    cK, cw2, ck = [V("col", 24 * i, 24 * i + NK) for i in range(3)]
+    fillc(V("nil", 0, 512), 0.0)
     cp(V("uo", 0, 8), V("k16", 0, 8))
     ts(V("pi", 2, 4), V("pi", 0, 2), 15, Op.bitwise_and)
-    fillc(V("win", 0, HA), 0.0)
-    cp(V("pf", 0, 2), V("pi", 2, 4))
-    qcol = V("pf", 0, 1)
-    fillc(V("win", HB - 128, HB), 0.0)
-    ts(V("md", 0, C), V("jt", 0, C), qcol, Op.is_equal, 2 * BIG, Op.mult)
+    ts(V("pi", 4, 6), V("pi", 0, 2), 2, Op.logical_shift_right, 3, Op.bitwise_and)
+    ts(V("pi", 6, 8), V("pi", 0, 2), 3, Op.bitwise_and)
     fillc(V("zt", 0, 128), 0.0)
     fillc(V("cn", 0, 96), 0.0)
-    fillc(V("gl", 2 * NK - 1, 2 * NK), 0.0)
-    fillc(V("ck", 0, KD), -LOW)
-    ts(V("c4", 0, NK), V("k16", 0, NK), qcol, Op.add, 4.0, Op.mult)
-    ts(V("ck", KD, NK), V("k16", KD, NK), 16.0 - LOW, Op.add)
-    ts(V("cw2", 0, NK), V("c4", 0, NK), 0.5, Op.mult, -1.0 * C, Op.add)
-    ts(V("c4", 24, 24 + NK), V("c4", 0, NK), 4.0 * A + SPAN, Op.add)
-    ts(V("c4", 0, NK), V("c4", 0, NK), 4.0 * A, Op.add)
+    cp(V("pf", 0, 6), V("pi", 2, 8))
+    fillc(V("pk", 24, 48), 0.0)
+    fillc(V("col", 48, 48 + NL), -16.0)
+    ts(V("md", 0, C), V("jt", 0, C), q16, Op.is_equal, 2 * BIG, Op.mult)
+    fillc(V("col", 48 + NL, 48 + NH), LOW)
+    fillc(V("col", 48 + NH, 48 + NK), 0.0)
+    quant(V("lq0", 0, 128), V("ls0", 0, 128), V("nil", 0, 512))
     act(V("r01", 0, C), V("jt", 0, C), Fn.Sign)
     act(V("rs", 0, C), V("r01", 0, C), Fn.Identity, bias=-BIG, scale=2 * BIG)
     act(V("md", 0, C), V("md", 0, C), Fn.Identity, bias=-BIG)
+    hold16, hold4 = V("hold", 0, A), V("hold", A, 2 * A)
+    for i, (j, q) in enumerate(((V("jt", 0, A), q16), (V("j4", 0, A), q4))):
+        ts(V("hold", A * i, A * i + A), j, q, Op.not_equal)
+        ts(V("hold", A * i + 2 * A, A * i + 3 * A), j, q, Op.subtract, 1.0, Op.is_equal)
+    ts(back16, q16, 15.0, Op.is_equal, 1 / JUMP, Op.max)
+    ts(V("hold", 2 * A, 4 * A), V("hold", 2 * A, 4 * A), JUMP, Op.mult)
+    ts(back4, q4, 3.0, Op.is_equal, 1 / JUMP, Op.max)
+    ts(cK, V("k16", 0, NK), q16, Op.add, float(OFF), Op.add)
+    tt(V("hold", 0, 2 * A), V("hold", 0, 2 * A), V("hold", 2 * A, 4 * A), Op.max)
+    ts(cw2, cK, 2.0, Op.mult, -2.0 * OFF - C, Op.add)
     quant(V("qu", 0, 128), V("su", 0, 128), V("ut", 0, 512))
     uo = V("uo", 0, 8)
     note("v", lambda e: e.tensor_copy(T.qur[:, 0:128].bitcast(dt.uint32), T.qu[:, 0:128].bitcast(dt.uint32).indirect(uo[0])), [V("qu", 0, 128), uo], [V("qur", 0, 128)])
     act(V("sur", 0, 128), ind(V("su", 0, 128), uo), Fn.Copy)
 
     QX, QE = ("qx", "sx"), ("qe", "se")
-    wr, spS, wp, spp, old, recv, t2, t3, t4, t5, some, sp, pw = [W(i) for i in range(13)]
+    at, wr, mine, mx, sp, old, cF, mf, cap, recv, wp, t5 = [W(i) for i in range(12)]
     for t in range(R):
-        H0, H1 = (HA, HB) if t % 2 == 0 else (HB, HA)
-        X0, X1 = H0 + 4 * A, H1 + 4 * A
-        small = V("win", H0, H0 + SPAN)
-        lo, hi = (HA, BH + (4 * A if t == 0 else SPAN)) if t % 2 == 0 else (AH, WEND)
+        win, nxt = "w%d" % t, "w%d" % (t + 1)
+        span = PAIR if t else A
+        DH = 4 * (PAIR + span - A)
+        whole = V(win, 0, DH + 4 * (span + A))
+        lq, ls, lm, lc = "lq%d" % t, "ls%d" % t, "lm%d" % t, "lc%d" % t
+        LH = C if t else 128
         if t == 0:
             for a in (0, HALF):
-                quant(V("qx", a, a + HALF), V("sx", a, a + HALF), V("win", X0 + 4 * a, X0 + 4 * a + 2 * C))
+                quant(V("qx", a, a + HALF), V("sx", a, a + HALF), V(win, 4 * a, 4 * a + 2 * C))
         else:
-            quant(V("qx", 0, C), V("sx", 0, C), V("win", X0, X0 + 4 * C))
+            quant(V("qx", 0, C), V("sx", 0, C), V(win, 0, 4 * C))
         mm(0, ("qur", "sur"), 0, QX, 0, C)
         mm(1, ("qur", "sur"), 0, QX, 0, C)
+        if t:
+            send(t, "ax%d" % t, V("qx", 0, C), V(lq, 0, C))
+            send(t, "ax%d" % t, V("sx", 0, C), V(ls, 0, C))
+            landed(t, "ax%d" % t, 2, [V(lq, 0, C), V(ls, 0, C)])
+            for b in range(4):
+                mm(4 + b, QE, 128 * b, (lq, ls), 0, C)
         if t == 1:
-            cp(V("cn", 24, 24 + NK), recv)
+            tt(W(12), cn(0), cn(1), Op.max)
+            rel = [rank, rank ^ STEP[0], rank ^ STEP[2], rank ^ STEP[1]]
+            for d3 in range(4):
+                iota(V("tab", 64 * d3, 64 * d3 + 64), [[4 ** rel[2], 4], [4 ** rel[1], 4], [4 ** rel[0], 4]], d3 * 4 ** rel[3], 0)
         if t == 2:
-            tt(V("cn", 72, 72 + NK), pw, recv, Op.mult)
-            tt(V("cn", 48, 48 + NK), V("lc1", 48, 48 + NK), recv, Op.mult)
             for i in range(1, 4):
                 digit(i, "cn", Fn.Copy)
-        if t:
-            lqx, lsx, lc = "lqx%d" % t, "lsx%d" % t, "lc%d" % t
-            send(t, "ax%d" % t, [(V("qx", 0, C), V(lqx, 0, C))])
-            send(t, "ax%d" % t, [(V("sx", 0, C), V(lsx, 0, C))])
-            if t == 1:
-                send(t, "ac1", [(V("cn", 0, NK), V(lc, 72, 72 + NK)), (V("cn", 24, 24 + NK), V(lc, 48, 48 + NK))])
-            else:
-                send(t, "ac2", [(V("cn", 0, 48), V(lc, 48, 96)), (V("cn", 48, 96), V(lc, 0, 48))])
-            landed(t, "ax%d" % t, 2, [V(lqx, 0, C), V(lsx, 0, C)])
-            landed(t, "ac%d" % t, 1, [V(lc, 0, 96)])
-            for b in range(4):
-                mm(4 + b, QE, 128 * b, (lqx, lsx), 0, C)
-        for a, b in ((16 * KS, C), (0, 16 * KS)):
-            tt(V("d1", a, b), V("ps", a, b), V("md", a, b), Op.min)
-            scan(V("fill", a, b), V("rs", a, b), V("d1", a, b), -BIG, Op.min, Op.max)
-        tt(V("eq", 0, C), V("ps", 0, C), V("fill", 0, C), Op.is_equal)
+        cuts = ((C - 64, C), (0, 128), (128, C - 64))
+        for i in range(len(cuts) + 1):
+            if i < len(cuts):
+                tt(V("d1", *cuts[i]), V("ps", *cuts[i]), V("md", *cuts[i]), Op.min)
+            if i:
+                scan(V("fill", *cuts[i - 1]), V("rs", *cuts[i - 1]), V("d1", *cuts[i - 1]), -BIG, Op.min, Op.max)
+        if t == 1:
+            tt(cF, W(12), cK, Op.min)
 
         def own(k):
             return V("fill", 16 * k + 15, 16 * k + 16)
 
-        def vec_cmp(k):
+        def fl(k, a, b):
+            return V("fl", ROW * k + a, ROW * k + b)
+
+        def earlier(k):
+            ts(fl(k, 0, 16 * k + 16), V("ps", 0, 16 * k + 16), own(k), Op.is_ge, -1.0, Op.mult)
+
+        def after(k):
             e = 16 * k + 16
-            ts(V("fl", C * k, C * k + e), V("ps", 0, e), own(k), Op.is_ge)
-            if k < KS:
-                ts(V("fl", C * k + e, C * k + C), V("ps", e, C), own(k), Op.is_gt)
+            if k < NH:
+                ts(fl(k, e, C), V("ps", e, C), own(k), Op.is_gt, -1.0, Op.mult)
+            elif e < C:
+                ts(fl(k, e, C), V("ps", e, C), own(k), Op.is_le)
 
-        def vec_sum(k):
-            h = HALF if k < KS else 8 * k + 8
-            scan(V("sc", HALF * (k + 1) - h, HALF * (k + 1)), V("fl", C * k, C * k + h), V("fl", C * k + h, C * k + 2 * h),
-                 V("gl", 2 * NK + k, 2 * NK + k + 1), Op.add, Op.add)
+        def total(k):
+            scan(V("sc", HALF * k, HALF * k + HALF), fl(k, 0, HALF), fl(k, HALF, C), fl(k, C, C + 1), Op.add, Op.add)
 
-        def act_cmp(k):
-            a = 0 if k > KS else 16 * k + 16
-            act(V("fl", C * k + a, C * k + C), V("ps", 512 + a, 512 + C), Fn.Sign, bias=own(k), scale=-1.0)
+        def sign(k):
+            a, b = (16 * k + 16, C) if k < NL else (0, 16 * k + 16)
+            act(fl(k, a, b), V("ps", 512 + a, 512 + b), Fn.Sign, bias=own(k), scale=-1.0)
 
-        def act_less(k):
-            x = V("fl", C * k, C * k + 16 * k + 16)
-            act(x, x, Fn.Relu, acc=V("gl", k, k + 1))
+        def count(k):
+            act(fl(k, 0, C + 1), fl(k, 0, C + 1), Fn.Relu, scale=-1.0 if k < NL else 1.0, acc=V("gl", k, k + 1))
 
-        def act_more(k):
-            if k + 1 < NK:
-                x = V("fl", C * k + 16 * k + 16, C * k + C)
-                act(x, x, Fn.Relu, scale=-1.0, acc=V("gl", NK + k, NK + k + 1))
-        vec_cmp(0)
-        scan(V("nu", 0, C), V("r01", 0, C), V("eq", 0, C), 0.0, Op.mult, Op.subtract)
-        vec_cmp(1)
-        tt(V("gl", 2 * NK, 3 * NK), V("nu", 15, C, 16), V("ck", 0, NK), Op.add)
-        for k in range(2, KD):
-            vec_cmp(k)
-            vec_sum(k - 2)
-        vec_sum(KD - 2)
-        vec_sum(KD - 1)
-        act_cmp(NK - 1)
-        for k in range(NK - 2, KD - 1, -1):
-            act_cmp(k)
-            act_less(k + 1)
-            if k > KD:
-                act_more(k + 1)
-        act_cmp(KS)
-        act_less(KD)
-        for k in (KD + 1, KD, KS):
-            act_more(k)
+        def places(a, b):
+            if a >= NH:
+                ts(V("pl", a, b), V("gl", a, b), -1.0, Op.mult, float(C), Op.add)
+            elif a >= NL:
+                ts(V("pl", a, b), V("sc", HALF * a + HALF - 1, HALF * b, HALF), -1.0, Op.mult, LOW, Op.add)
+            else:
+                ts(V("pl", a, b), V("gl", a, b), -16.0, Op.add)
+
+        def spread(a, b):
+            cp(ind(V("ew", 0, C), V("pl", a, b)), V("i4", 16 * a, 16 * b))
+        after(NK - 2)
+        tt(V("eq", 0, C), V("ps", 0, C), V("fill", 0, C), Op.is_equal)
+        after(NK - 3)
+        after(NK - 4)
+        scan(V("nu", 0, C), V("r01", 0, C), V("eq", 0, C), 0.0, Op.mult, Op.add)
+        for k in range(NK - 5, NH - 1, -1):
+            after(k)
+        tt(V("fl", C, ROW * NK, ROW), V("nu", 15, C, 16), ck, Op.add)
+        for k in range(NL):
+            earlier(k)
+        for k in range(NK - 1, NH - 1, -1):
+            sign(k)
+        for k in range(NK - 1, NH - 1, -1):
+            count(k)
+        low = list(range(4, NL)) + list(range(4))
+        for k in low:
+            sign(k)
+        for k in low:
+            count(k)
+        between = {NH - 3: [lambda: places(NH, NK)]}
+        if t == 2:
+            between[NH - 8] = [lambda: tt(V("df", 0, 48), cn(0, 48), V(lc, 48, 96), Op.subtract)]
+            between[NH - 7] = [lambda: tt(V("df", 48, 96), cn(2, 48), V(lc, 0, 48), Op.subtract)]
+            between[NH - 6] = [lambda: tt(W(12), V("df", 0, NK), V("df", 24, 24 + NK), Op.max)]
+            between[NH - 5] = [lambda: tt(W(12), W(12), V("df", 72, 72 + NK), Op.max)]
+            between[NH - 4] = [lambda: tt(cF, W(12), cK, Op.min)]
+        for k in range(NL, NH):
+            earlier(k)
+            after(k)
+            if k > NL:
+                total(k - 1)
+            for f in between.get(k, []):
+                f()
+        places(4, NL)
+        total(NH - 1)
+        spread(NH, NK)
+        places(NL, NH)
+        places(0, 2)
+        spread(4, NH)
+        places(2, 4)
+        pl = V("pl", 0, NK)
+
+        def dcol(b):
+            if t:
+                act(V(win, 4 * PAIR + b, DH, 4), V("ps", 512 * (4 + b), 512 * (4 + b) + C), Fn.Copy, scale=2.0)
+        dcol(0)
+        dcol(1)
+        spread(0, 4)
+        ts(at, pl, float(OFF + C), Op.add)
+        ts(wr, pl, float(A), Op.is_lt, ONE, Op.mult)
+        scan(V("eh", 0, A), hold4, V("ew", 0, A), 0.0, Op.mult, Op.add)
+        scan(V("eh", A, 2 * A), hold16, V("ew", 0, A), 0.0, Op.mult, Op.add)
+        ts(V("zl", 0, 24), V("eh", 3, A, 4), back4, Op.mult, b4, Op.add)
+        tt(mine, at, wr, Op.min)
+        ts(V("ml", NK, NK + 6), V("eh", A + 15, 2 * A, 16), back16, Op.mult, 0.25, Op.mult)
+        offer = mx if t else mine
         if t:
-            for b in range(4):
-                act(V("win", AH + 4 * A + b, BH, 4), V("ps", 512 * (4 + b), 512 * (4 + b) + C), Fn.Copy, scale=2.0)
-        tt(V("sc", HALF * KD + HALF - 1, HALF * NK, HALF), V("gl", 2 * NK + KD, 3 * NK), V("gl", KD, NK), Op.subtract)
-        x = V("sc", HALF * KS + HALF - 1, HALF * NK, HALF)
-        tt(x, x, V("gl", NK + KS, 2 * NK), Op.add)
-        pl, lp, le = V("pl", 0, NK), V("lp%d" % t, 0, NK), V("le%d" % t, 0, 6)
-        ts(pl, V("sc", HALF - 1, HALF * NK, HALF), LOW, Op.add)
-        send(t, "ap%d" % t, [(pl, lp)])
-        landed(t, "ap%d" % t, 1, [lp])
-        cp(ind(V("ew", 0, C), pl), V("i4", 0, C))
-        tt(V("d1", 0, A), V("ew", 0, A), V("md", 0, A), Op.min)
-        scan(V("fill", 0, A), V("rs", 0, A), V("d1", 0, A), -BIG, Op.min, Op.max)
-        for b in (1, 2, 3, 0):
-            ts(V("eo", 6 * b, 6 * b + 6), V("fill", 15, A, 16), float(b), Op.add)
-        for b in (1, 2, 3, 0):
-            move("a" if b else "v", V("zt", 128 + b, 512, 4), ind(V("win", X0, X0 + 4 * C), V("eo", 6 * b, 6 * b + 6)))
-        send(t, "ae%d" % t, [(V("eo", 0, 6), le)])
-        landed(t, "ae%d" % t, 1, [le])
-        mine, theirs = slot(sp, pl, 13, 0), slot(spp, lp, 15, AH - lo)
-        mine[0]()
-        mine[1]()
+            tt(mx, mine, cF, Op.max)
+        for q, a, b in (("a", 10, 24), ("v", 0, 10)):
+            move(q, V("zt", 128 + 16 * a, 128 + 16 * b), ind(V(win, 0, 4 * C), V("zl", a, b)))
+        cp(V("ml", 0, NK), offer)
+        send(t, "am%d" % t, V("ml", 0, 28), V(lm, 0, 28))
+        landed(t, "am%d" % t, 1, [V(lm, 0, 28)])
         quant(V("qz", 0, 128), V("sz", 0, 128), V("zt", 0, 512))
         for b in range(4):
             mm(b, ("qw", "sw"), 128 * b, ("qz", "sz"), 0, 128)
+        dcol(2)
+        tt(sp, mine, cK, Op.max)
+        tt(cn(0), cn(0), wr, Op.add)
+        ts(old, offer, 0.0, Op.is_gt, float(span), Op.mult)
 
         def spo(b, make=False):
             if make:
-                ts(spo(b), sp, float(b), Op.add)
+                ts(spo(b), sp, 4.0, Op.mult, b - 4.0 * OFF, Op.add)
             return V("so", NK * b, NK * b + NK)
-        mine[2]()
-        ts(wr, pl, float(A), Op.is_lt)
-        mine[3]()
-        tt(V("cn", 0, NK), V("cn", 0, NK), wr, Op.add)
         spo(0, True)
+        spo(1, True)
         for b in range(4):
             act(V("rl", A * b, A * b + A), V("ps", 512 * b + 32, 512 * b + 128), Fn.Relu, scale=0.03125)
-            tt(V("win", H0 + b, X0, 4), V("rl", A * b, A * b + A), V("zt", 128 + b, 512, 4), Op.add)
-        quant(V("qh", 0, 128), V("sh", 0, 128), V("win", H0 - 128, X0))
-        lqh, lsh = "lqh%d" % t, "lsh%d" % t
-        send(t, "ah%d" % t, [(V("qh", 32, 128), V(lqh, 0, A))])
-        send(t, "ah%d" % t, [(V("sh", 32, 128), V(lsh, 0, A))])
+            tt(V(win, 4 * C + b, 4 * PAIR, 4), V("rl", A * b, A * b + A), V("zt", 128 + b, 512, 4), Op.add)
+        dcol(3)
+        if t == 2:
+            digit(0, "cn", Fn.Copy)
+            for i in range(1, 4):
+                digit(i, "df", Fn.Relu)
+        quant(V("qh", 0, 128), V("sh", 0, 128), V(win, 4 * PAIR - 512, 4 * PAIR))
+        send(t, "ah%d" % t, V("qh", 32, 128), V(lq, LH, LH + A))
+        send(t, "ah%d" % t, V("sh", 32, 128), V(ls, LH, LH + A))
+        them, ep = V(lm, 0, NK), V(lm, NK, NK + 6)
 
         def half(b, q):
-            if q == "v":
-                ts(V("xh", C * b, C * b + C), ind(small, spo(b)), 0.5, Op.mult)
-            else:
-                act(V("xh", C * b, C * b + C), ind(small, spo(b)), Fn.Copy, scale=0.5)
+            move(q, V("xh", C * b, C * b + C), ind(V(win, 0, 4 * PAIR), spo(b)), 0.5)
 
         def mean(b):
-            tt(V("win", BH + 4 * A + b, BH + SPAN, 4), V("ps", 512 * (4 + b), 512 * (4 + b) + C), V("xh", C * b, C * b + C), Op.add)
+            tt(V(win, 8 * PAIR + b, 8 * PAIR + 4 * C, 4), V("ps", 512 * (4 + b), 512 * (4 + b) + C), V("xh", C * b, C * b + C), Op.add)
 
         def owns(b):
             act(V("oh", A * b, A * b + A), ind(V("xh", C * b, C * b + C), ep), Fn.Copy)
-        ep, wantu = V("wu", 0, 6), V("wu", 8, 8 + NK)
-        if t == 2:
-            digit(0, "cn", Fn.Copy)
+
+        def offsets():
+            for b in range(4):
+                ts(V("fo", NK * b, NK * b + NK), t5, 4.0, Op.mult, b - 4.0 * OFF, Op.add)
         half(0, "a")
-        spo(1, True)
-        half(1, "a")
+        spo(2, True)
+        spo(3, True)
         if t == 0:
-            spo(2, True)
-            spo(3, True)
+            iota(V("any", 0, 16), [[0, 16]], 0, 0)
+            iota(V("any", 16, 3 * PAIR), [[0, 3 * PAIR - 16]], 1, 0)
+            half(1, "a")
             half(2, "v")
-            half(3, "a")
-            fillc(V("win", AH + 4 * A, BH), 0.0)
+            half(3, "v")
             quant(V("qe", 0, 512), V("se", 0, 512), et)
-            theirs[0]()
-            theirs[1]()
-            ts(ep, le, 0.25, Op.mult)
-            for i in range(R):
-                quant(V("lqh%d" % i, A, A + 128), V("lsh%d" % i, A, A + 128), V("win", AH + 4 * A, AH + 4 * A + 512))
-            theirs[2]()
-            ts(old, wr, float(SPAN), Op.mult)
-            theirs[3]()
-            ts(recv, lp, float(A), Op.is_lt)
+            ts(mf, them, float(span), Op.add)
+            ts(cn(1), them, 0.0, Op.is_gt, ONE, Op.mult)
+            tt(mf, mf, old, Op.add)
             for b in range(4):
                 owns(b)
-            tt(t2, spp, old, Op.add)
-            fillc(V("pk", 24, 48), 0.0)
-            tt(t3, t2, sp, Op.subtract)
-        else:
-            ts(wp, lp, float(A), Op.is_lt)
-            if t == 1:
-                spo(2, True)
-                tt(pw, V(lc, 72, 72 + NK), wp, Op.add)
-                spo(3, True)
-                tt(some, pw, V(lc, 48, 48 + NK), Op.add)
-            else:
-                tt(V("df", 0, 96), V(lc, 0, 96), V("cn", 0, 96), Op.subtract)
-                spo(2, True)
-                tt(W(17), V("df", 24, 24 + NK), V("df", 72, 72 + NK), Op.max)
-                tt(V("df", 48, 48 + NK), V("df", 48, 48 + NK), wp, Op.add)
-                spo(3, True)
-                tt(some, W(17), V("df", 48, 48 + NK), Op.max)
-            theirs[0]()
-            ts(wantu, some, 0.0, Op.is_gt)
-            act(V("row", 0, C), ind(V("i4", 0, 16), wantu), Fn.Copy)
-            theirs[1]()
-            mean(0)
-            theirs[2]()
-            if t == 1:
-                tt(W(18), V("cn", 0, NK), V("cn", 24, 24 + NK), Op.add)
-            else:
-                tt(W(18, 48), V("df", 0, 48), V("df", 48, 96), Op.min)
-            theirs[3]()
-            scan(V("row", C, 2 * C), V("row", 0, C), V("row", 0, C), 0.0, Op.add, Op.max)
-            half(2, "a")
-            act(V("row", 2 * C, 3 * C), V("row", C, 2 * C), Fn.Sign, bias=4.0 * K + 2.0, scale=-1.0, acc=V("acc", 0, 1))
-            half(3, "a")
-            if t == 1:
-                ts(spS, sp, float(H0 - lo), Op.add)
-                ts(some, some, 0.0, Op.is_gt)
-                ts(old, W(18), 0.0, Op.is_gt, float(SPAN), Op.mult)
-            else:
-                tt(W(18), W(18), W(19), Op.min)
-                ts(some, some, 0.0, Op.is_gt)
-                ts(old, W(18), 0.0, Op.is_lt, float(SPAN), Op.mult)
-            mean(1)
-            tt(t2, spp, old, Op.add)
-            ts(ep, le, 0.25, Op.mult)
-            tt(t3, t2, spS if t == 1 else sp, Op.subtract)
-            for b in range(4):
-                owns(b)
-            ts(W(17), V("cw2", 0, NK), V("acc", 0, 1), Op.is_lt)
-            tt(t3, t3, some, Op.mult)
-            mean(2)
-        tt(t4, t3, recv if t == 0 else W(17), Op.mult)
-        if t:
-            tt(recv, W(17), some, Op.mult)
-        else:
             quant(V("qv", 0, 128), V("sv", 0, 128), V("vt", 0, 512))
-        tt(t5, t4, spS if t == 1 else sp, Op.add)
-        if t:
-            mean(3)
-        for b in range(4):
-            ts(V("fo", NK * b, NK * b + NK), t5, float(b), Op.add)
-        steps = []
-        if t == 2:
-            for i in range(1, 4):
-                digit(i, "df", Fn.Relu)
-            steps = [lambda: tt(W(20, 96), V("pk", 0, 96), V("pk", 96, 192), Op.add),
-                     lambda: tt(W(20, 48), W(20, 48), W(22, 48), Op.add),
-                     lambda: tt(W(21), W(21), recv, Op.mult),
-                     lambda: tt(W(20), W(20), W(21), Op.add)]
-        landed(t, "ah%d" % t, 2, [V(lqh, 0, A), V(lsh, 0, A)])
-        for b in range(4):
-            mm(b, QE, 128 * b, (lqh, lsh), 0, 128)
-        for b in range(4):
-            tt(V("win", BH + b, BH + 4 * A, 4), V("ps", 512 * b, 512 * b + A), V("oh", A * b, A * b + A), Op.add)
-            act(V("win", AH + b, AH + 4 * A, 4), V("ps", 512 * b, 512 * b + A), Fn.Copy, scale=2.0)
-        if steps:
+            tt(t5, mf, sp, Op.max)
+            offsets()
+        else:
+            half(1, "a")
+            half(3, "v")
+            act(V("row", 0, C), ind(V("any", 0, 3 * PAIR), them), Fn.Copy)
+            mean(0)
+            half(2, "v")
+            ts(mf, them, float(span), Op.add)
+            if t == 1:
+                ts(wp, them, float(OFF + C), Op.is_ge, ONE, Op.mult)
+                steps = [lambda: None,
+                         lambda: tt(wp, wp, V(lc, 0, NK), Op.add),
+                         lambda: tt(cn(2), V(lc, 24, 24 + NK), recv, Op.min),
+                         lambda: tt(cn(3), wp, recv, Op.min)]
+            else:
+                ts(V("pk", 24, 24 + NK), them, float(OFF + C), Op.is_ge, 16.0, Op.mult)
+                steps = [lambda: tt(W(14, 96), V("pk", 0, 96), V("pk", 96, 192), Op.add),
+                         lambda: tt(W(14, 48), W(14, 48), W(16, 48), Op.add),
+                         lambda: tt(W(15), W(15), recv, Op.min),
+                         lambda: tt(W(14), W(14), W(15), Op.add)]
+            tt(mf, mf, old, Op.add)
             steps[0]()
+            scan(V("row", C, 2 * C), V("row", 0, C), V("row", 0, C), 0.0, Op.add, Op.max)
+            act(V("row", 2 * C, 3 * C), V("row", C, 2 * C), Fn.Sign, bias=K + 0.5, scale=-1.0, acc=V("acc", 0, 1))
+            for b in (0, 3, 1, 2):
+                owns(b)
             steps[1]()
+            mean(3)
+            ts(cap, cw2, V("acc", 0, 1), Op.is_ge, -ONE, Op.mult)
+            mean(1)
+            tt(mf, mf, cap, Op.add)
+            mean(2)
+            tt(t5, mf, sp, Op.max)
+            ts(recv, mf, float(OFF), Op.is_gt, 4 * ONE, Op.mult)
+            offsets()
+            steps[2]()
+            steps[3]()
+        if t + 1 < R:
+            send(t + 1, "ac%d" % (t + 1), cn(0, 48 * t + 48), V("lc%d" % (t + 1), 0, 48 * t + 48))
+            landed(t + 1, "ac%d" % (t + 1), 1, [V("lc%d" % (t + 1), 0, 48 * t + 48)])
+        landed(t, "ah%d" % t, 2, [V(lq, LH, LH + A), V(ls, LH, LH + A)])
+        for b in range(4):
+            mm(b, QE, 128 * b, (lq, ls), LH - 32, 128)
+        for i, b in enumerate((0, 1, 2, 3, 1, 0, 3, 2)):
+            d = V("ps", 512 * b + 32, 512 * b + 128)
+            if i % 2:
+                tt(V(win, DH + 4 * span + b, DH + 4 * (span + A), 4), d, V("oh", A * b, A * b + A), Op.add)
+            else:
+                act(V(win, DH + b, DH + 4 * A, 4), d, Fn.Copy, scale=2.0)
         if t + 1 < R:
             for b in range(4):
-                move("v" if b < 2 else "a", V("win", X1 + b, X1 + 4 * C, 4), ind(V("win", lo, hi), V("fo", NK * b, NK * b + NK)))
-    runs = ((0, 12), (12, NK))
-    for i, (k0, k1) in enumerate(runs):
-        a, z = 16 * k0, 16 * k1
-        for b in range(4):
-            move("v" if b < 2 else "a", V("win", X1 + 4 * a + b, X1 + 4 * z, 4), ind(V("win", lo, hi), V("fo", NK * b + k0, NK * b + k1)))
-        steps[2 + i]()
-        quant(V("qx", a, z), V("sx", a, z), V("win", X1 + 4 * a, X1 + 4 * z))
+                move("v" if b < 2 else "a", V(nxt, b, 4 * C, 4), ind(whole, V("fo", NK * b, NK * b + NK)))
+    runs = ((0, 14), (14, NK))
+
+    def gather(i, b):
+        k0, k1 = runs[i]
+        move("v" if b < 2 else "a", V(nxt, 64 * k0 + b, 64 * k1, 4), ind(whole, V("fo", NK * b + k0, NK * b + k1)))
+
+    def pack(i):
+        a, z = 16 * runs[i][0], 16 * runs[i][1]
+        quant(V("qx", a, z), V("sx", a, z), V(nxt, 4 * a, 4 * z))
         mm(i, ("qv", "sv"), 0, QX, a, z - a)
         dma("s", T.oc[:, 4 * a:4 * z], T.qx[:, a:z].bitcast(dt.uint8), [V("qx", a, z)], [])
-    cp(V("wu", 32, 32 + NK), W(20))
-    cp(V("ovr", 0, C), ind(V("tab", 0, 256), V("wu", 32, 32 + NK)))
-    for i, (k0, k1) in enumerate(runs):
-        a, z = 16 * k0, 16 * k1
-        act(V("yt", a, z), V("ps", 512 * i, 512 * i + z - a), Fn.Copy)
+
+    def result(i, q):
+        a, z = 16 * runs[i][0], 16 * runs[i][1]
+        move(q, V("yt", a, z), V("ps", 512 * i, 512 * i + z - a))
         dma("a", T.y[:, a:z], T.yt[:, a:z], [V("yt", a, z)], [])
+    cp(V("wu", 0, NK), W(14))
+    for i, b in ((0, 0), (0, 2), (0, 1), (0, 3), (1, 0), (1, 2), (1, 3)):
+        gather(i, b)
+    pack(0)
+    gather(1, 1)
+    pack(1)
+    result(0, "a")
     for k in range(4):
         dma("s", T.osc[4 * k:4 * k + 4, :], T.sx[32 * k:32 * k + 4, :], [V("sx", 0, C)], [])
+    cp(V("ovr", 0, C), ind(V("tab", 0, 256), V("wu", 0, NK)))
     dma("s", T.ov[:], T.ovr[0:128:16, :], [V("ovr", 0, C)], [])
+    result(1, "a")
     emit()

@@ -4,7 +4,8 @@ from concourse.mybir import dt, AluOpType, ActivationFunctionType
 C, A, K, R = 352, 96, 160, 3
 STEP = [1, 6, 7]
 NK = C // 16
-NL, NH = 5, 16
+NL, NH = 4, 16
+MID = NL + 2
 HALF = C // 2
 ROW = C + 2
 BIG = 2.0 ** 96
@@ -27,20 +28,20 @@ SCRATCH = {
     "qz": ("sbuf", [128, 128], F8), "sz": ("sbuf", [128, 128], U8), "qh": ("sbuf", [128, 128], F8), "sh": ("sbuf", [128, 128], U8),
     "pi": ("sbuf", [128, 8], I32), "pf": ("sbuf", [128, 8], F32), "k16": ("sbuf", [128, NK], F32), "uo": ("sbuf", [128, 8], U16),
     "jt": ("sbuf", [128, C], F32), "md": ("sbuf", [128, C], F32), "rs": ("sbuf", [128, C], F32), "r01": ("sbuf", [128, C], BF),
-    "i4": ("sbuf", [128, C], F32), "j4": ("sbuf", [128, A], F32), "hold": ("sbuf", [128, 4 * A], F32), "col": ("sbuf", [128, 72], F32),
+    "i4": ("sbuf", [128, C], F32), "j4": ("sbuf", [128, A], F32), "hold": ("sbuf", [128, 2 * A], F32), "col": ("sbuf", [128, 72], F32),
     "tab": ("sbuf", [128, 256], F32), "any": ("sbuf", [128, 3 * PAIR], BF),
     "d1": ("sbuf", [128, C], F32), "fill": ("sbuf", [128, C], F32), "eq": ("sbuf", [128, C], BF), "nu": ("sbuf", [128, C], BF),
     "fl": ("sbuf", [128, ROW * NK], BF), "sc": ("sbuf", [128, HALF * NK], BF), "gl": ("sbuf", [128, NK], F32),
-    "pl": ("sbuf", [128, NK], U16), "ew": ("sbuf", [128, C], F32), "eh": ("sbuf", [128, 2 * A], F32), "zl": ("sbuf", [128, 24], U16),
-    "ml": ("sbuf", [128, 28], U16), "so": ("sbuf", [128, 4 * NK], U16),
-    "cn": ("sbuf", [128, 96], BF), "df": ("sbuf", [128, 96], F32), "w": ("sbuf", [128, 24 * 20], F32), "wu": ("sbuf", [128, NK], U16),
+    "pl": ("sbuf", [128, NK], U16), "ew": ("sbuf", [128, C], F32), "eh": ("sbuf", [128, 2 * A], F32),
+    "ml": ("sbuf", [128, 52], U16), "so": ("sbuf", [128, 4 * NK], U16),
+    "cn": ("sbuf", [128, 96], BF), "df": ("sbuf", [128, 96], F32), "w": ("sbuf", [128, 24 * 18], F32), "wu": ("sbuf", [128, NK], U16),
     "fo": ("sbuf", [128, 4 * NK], U16), "row": ("sbuf", [128, 3 * C], BF), "acc": ("sbuf", [128, 2], F32),
-    "pk": ("sbuf", [128, 192], F32), "ovr": ("sbuf", [128, C], F32),
+    "pk": ("sbuf", [128, 96], F32), "ovr": ("sbuf", [128, C], F32),
 }
 for _t in range(R):
     SCRATCH["lq%d" % _t] = ("sbuf", [128, (C if _t else 128) + A], F8)
     SCRATCH["ls%d" % _t] = ("sbuf", [128, (C if _t else 128) + A], U8)
-    SCRATCH["lm%d" % _t] = ("sbuf", [128, 28], U16)
+    SCRATCH["lm%d" % _t] = ("sbuf", [128, 46], U16)
     if _t:
         SCRATCH["lc%d" % _t] = ("sbuf", [128, 48 * _t], BF)
 SEMAPHORES = ["cv", "ca", "ct", "cg"] + ["a%s%d" % (k, t) for k in "hmxc" for t in range(R) if t or k in "hm"] + ["d%d" % i for i in range(44)]
@@ -190,9 +191,9 @@ def rank_program(g, core, T, topo):
     def cn(i, n=NK):
         return V("cn", 24 * i, 24 * i + n)
 
-    def digit(i, src, f):
-        at = 48 * i + (24 if f == Fn.Relu else 0)
-        act(V("pk", at, at + 24), V(src, 24 * i, 24 * i + 24), f, scale=(-1.0 if f == Fn.Relu else 1.0) * 4.0 ** i / ONE)
+    rel = [rank, rank ^ STEP[0], rank ^ STEP[2], rank ^ STEP[1]]
+    four = sorted(rel)
+    unit = [ONE * 4 ** four.index(r) for r in rel]
 
     dma("s", T.ut[:], T.u[:], [], [V("ut", 0, 512)])
     dma("a", T.w0[:, 0:2 * C], T.x[:, 0:2 * C], [], [V("w0", 0, 2 * C)])
@@ -211,37 +212,33 @@ def rank_program(g, core, T, topo):
     note("g", lambda e: e.affine_select(et[0], et[0], [[-1, 4], [1, 512]], Op.not_equal, 0.5, 0, -4), [et], [et])
     q16, q4, b4, back16, back4 = [V("pf", i, i + 1) for i in (0, 2, 4, 6, 7)]
     cK, cw2, ck = [V("col", 24 * i, 24 * i + NK) for i in range(3)]
-    fillc(V("nil", 0, 512), 0.0)
     cp(V("uo", 0, 8), V("k16", 0, 8))
     ts(V("pi", 2, 4), V("pi", 0, 2), 15, Op.bitwise_and)
     ts(V("pi", 4, 6), V("pi", 0, 2), 2, Op.logical_shift_right, 3, Op.bitwise_and)
     ts(V("pi", 6, 8), V("pi", 0, 2), 3, Op.bitwise_and)
+    fillc(V("col", 48, 48 + NL), -16.0)
+    cp(V("pf", 0, 6), V("pi", 2, 8))
+    fillc(V("col", 48 + NL, 48 + NH), LOW)
+    ts(V("md", 0, C), V("jt", 0, C), q16, Op.is_equal, 2 * BIG, Op.mult)
+    fillc(V("col", 48 + NH, 48 + NK), 0.0)
+    ts(back16, q16, 15.0, Op.is_equal, 1 / JUMP, Op.max)
+    ts(back4, q4, 3.0, Op.is_equal, 1 / JUMP, Op.max)
+    ts(cK, V("k16", 0, NK), q16, Op.add, float(OFF), Op.add)
     fillc(V("zt", 0, 128), 0.0)
     fillc(V("cn", 0, 96), 0.0)
-    cp(V("pf", 0, 6), V("pi", 2, 8))
-    fillc(V("pk", 24, 48), 0.0)
-    fillc(V("col", 48, 48 + NL), -16.0)
-    ts(V("md", 0, C), V("jt", 0, C), q16, Op.is_equal, 2 * BIG, Op.mult)
-    fillc(V("col", 48 + NL, 48 + NH), LOW)
-    fillc(V("col", 48 + NH, 48 + NK), 0.0)
-    quant(V("lq0", 0, 128), V("ls0", 0, 128), V("nil", 0, 512))
     act(V("r01", 0, C), V("jt", 0, C), Fn.Sign)
     act(V("rs", 0, C), V("r01", 0, C), Fn.Identity, bias=-BIG, scale=2 * BIG)
     act(V("md", 0, C), V("md", 0, C), Fn.Identity, bias=-BIG)
-    hold16, hold4 = V("hold", 0, A), V("hold", A, 2 * A)
-    for i, (j, q) in enumerate(((V("jt", 0, A), q16), (V("j4", 0, A), q4))):
-        ts(V("hold", A * i, A * i + A), j, q, Op.not_equal)
-        ts(V("hold", A * i + 2 * A, A * i + 3 * A), j, q, Op.subtract, 1.0, Op.is_equal)
-    ts(back16, q16, 15.0, Op.is_equal, 1 / JUMP, Op.max)
-    ts(V("hold", 2 * A, 4 * A), V("hold", 2 * A, 4 * A), JUMP, Op.mult)
-    ts(back4, q4, 3.0, Op.is_equal, 1 / JUMP, Op.max)
-    ts(cK, V("k16", 0, NK), q16, Op.add, float(OFF), Op.add)
-    tt(V("hold", 0, 2 * A), V("hold", 0, 2 * A), V("hold", 2 * A, 4 * A), Op.max)
-    ts(cw2, cK, 2.0, Op.mult, -2.0 * OFF - C, Op.add)
+    hold16, hold4, hold = V("hold", 0, A), V("hold", A, 2 * A), V("hold", 0, 2 * A)
+    act(hold16, V("jt", 0, A), Fn.Abs, bias=q16, scale=-1.0)
+    act(hold4, V("j4", 0, A), Fn.Abs, bias=q4, scale=-1.0)
     quant(V("qu", 0, 128), V("su", 0, 128), V("ut", 0, 512))
     uo = V("uo", 0, 8)
     note("v", lambda e: e.tensor_copy(T.qur[:, 0:128].bitcast(dt.uint32), T.qu[:, 0:128].bitcast(dt.uint32).indirect(uo[0])), [V("qu", 0, 128), uo], [V("qur", 0, 128)])
     act(V("sur", 0, 128), ind(V("su", 0, 128), uo), Fn.Copy)
+    act(hold, hold, Fn.Relu, bias=2.0, scale=-1.0)
+    act(hold, hold, Fn.Abs, bias=-3.0, scale=4.0)
+    act(hold, hold, Fn.Relu, bias=1.5 * JUMP - 0.5, scale=0.5 - JUMP / 2)
 
     QX, QE = ("qx", "sx"), ("qe", "se")
     at, wr, mine, mx, sp, old, cF, mf, cap, recv, wp, t5 = [W(i) for i in range(12)]
@@ -260,27 +257,34 @@ def rank_program(g, core, T, topo):
         mm(0, ("qur", "sur"), 0, QX, 0, C)
         mm(1, ("qur", "sur"), 0, QX, 0, C)
         if t:
+            tt(cn(0), cn(0), wr, Op.add)
+        if t == 1:
+            ts(cn(1), them, 0.0, Op.is_gt, unit[1], Op.mult)
+        if t == 2:
+            ts(wp, them, float(OFF + C), Op.is_ge, unit[3], Op.mult)
+            ts(recv, mf, float(OFF), Op.is_gt, 256 * ONE, Op.mult)
+            tt(wp, wp, V("lc1", 0, NK), Op.add)
+            tt(cn(2), V("lc1", 24, 24 + NK), recv, Op.min)
+            tt(cn(3), wp, recv, Op.min)
+        if t:
+            CL = 46 if t == 1 else 96
             send(t, "ax%d" % t, V("qx", 0, C), V(lq, 0, C))
+            send(t, "ac%d" % t, cn(0, CL), V(lc, 0, CL))
             send(t, "ax%d" % t, V("sx", 0, C), V(ls, 0, C))
+            landed(t, "ac%d" % t, 1, [V(lc, 0, CL)])
             landed(t, "ax%d" % t, 2, [V(lq, 0, C), V(ls, 0, C)])
             for b in range(4):
                 mm(4 + b, QE, 128 * b, (lq, ls), 0, C)
         if t == 1:
             tt(W(12), cn(0), cn(1), Op.max)
-            rel = [rank, rank ^ STEP[0], rank ^ STEP[2], rank ^ STEP[1]]
             for d3 in range(4):
-                iota(V("tab", 64 * d3, 64 * d3 + 64), [[4 ** rel[2], 4], [4 ** rel[1], 4], [4 ** rel[0], 4]], d3 * 4 ** rel[3], 0)
-        if t == 2:
-            for i in range(1, 4):
-                digit(i, "cn", Fn.Copy)
-        cuts = ((C - 64, C), (0, 128), (128, C - 64))
-        for i in range(len(cuts) + 1):
-            if i < len(cuts):
-                tt(V("d1", *cuts[i]), V("ps", *cuts[i]), V("md", *cuts[i]), Op.min)
-            if i:
-                scan(V("fill", *cuts[i - 1]), V("rs", *cuts[i - 1]), V("d1", *cuts[i - 1]), -BIG, Op.min, Op.max)
-        if t == 1:
-            tt(cF, W(12), cK, Op.min)
+                iota(V("tab", 64 * d3, 64 * d3 + 64), [[4 ** four[2], 4], [4 ** four[1], 4], [4 ** four[0], 4]], d3 * 4 ** four[3], 0)
+
+        def diag(a, b):
+            tt(V("d1", a, b), V("ps", a, b), V("md", a, b), Op.min)
+
+        def keep(a, b):
+            scan(V("fill", a, b), V("rs", a, b), V("d1", a, b), -BIG, Op.min, Op.max)
 
         def own(k):
             return V("fill", 16 * k + 15, 16 * k + 16)
@@ -295,7 +299,7 @@ def rank_program(g, core, T, topo):
             e = 16 * k + 16
             if k < NH:
                 ts(fl(k, e, C), V("ps", e, C), own(k), Op.is_gt, -1.0, Op.mult)
-            elif e < C:
+            else:
                 ts(fl(k, e, C), V("ps", e, C), own(k), Op.is_le)
 
         def total(k):
@@ -318,174 +322,174 @@ def rank_program(g, core, T, topo):
 
         def spread(a, b):
             cp(ind(V("ew", 0, C), V("pl", a, b)), V("i4", 16 * a, 16 * b))
-        after(NK - 2)
-        tt(V("eq", 0, C), V("ps", 0, C), V("fill", 0, C), Op.is_equal)
-        after(NK - 3)
-        after(NK - 4)
-        scan(V("nu", 0, C), V("r01", 0, C), V("eq", 0, C), 0.0, Op.mult, Op.add)
-        for k in range(NK - 5, NH - 1, -1):
-            after(k)
-        tt(V("fl", C, ROW * NK, ROW), V("nu", 15, C, 16), ck, Op.add)
-        for k in range(NL):
-            earlier(k)
-        for k in range(NK - 1, NH - 1, -1):
-            sign(k)
-        for k in range(NK - 1, NH - 1, -1):
-            count(k)
-        low = list(range(4, NL)) + list(range(4))
-        for k in low:
-            sign(k)
-        for k in low:
-            count(k)
-        between = {NH - 3: [lambda: places(NH, NK)]}
-        if t == 2:
-            between[NH - 8] = [lambda: tt(V("df", 0, 48), cn(0, 48), V(lc, 48, 96), Op.subtract)]
-            between[NH - 7] = [lambda: tt(V("df", 48, 96), cn(2, 48), V(lc, 0, 48), Op.subtract)]
-            between[NH - 6] = [lambda: tt(W(12), V("df", 0, NK), V("df", 24, 24 + NK), Op.max)]
-            between[NH - 5] = [lambda: tt(W(12), W(12), V("df", 72, 72 + NK), Op.max)]
-            between[NH - 4] = [lambda: tt(cF, W(12), cK, Op.min)]
-        for k in range(NL, NH):
-            earlier(k)
-            after(k)
-            if k > NL:
-                total(k - 1)
-            for f in between.get(k, []):
-                f()
-        places(4, NL)
-        total(NH - 1)
-        spread(NH, NK)
-        places(NL, NH)
-        places(0, 2)
-        spread(4, NH)
-        places(2, 4)
-        pl = V("pl", 0, NK)
+
+        def wanted(i):
+            if t == 1 and i == 0:
+                tt(cF, W(12), cK, Op.min)
+            if t == 2 and i == 0:
+                tt(V("df", 0, 48), cn(0, 48), V(lc, 48, 96), Op.subtract)
+                tt(V("df", 48, 96), cn(2, 48), V(lc, 0, 48), Op.subtract)
+            if t == 2 and i == 1:
+                tt(W(12), V("df", 0, NK), V("df", 24, 24 + NK), Op.max)
+                tt(W(13), V("df", 72, 72 + NK), cK, Op.min)
+            if t == 2 and i == 2:
+                tt(W(12), W(12), cK, Op.min)
+            if t == 2 and i == 3:
+                tt(cF, W(12), W(13), Op.max)
 
         def dcol(b):
             if t:
                 act(V(win, 4 * PAIR + b, DH, 4), V("ps", 512 * (4 + b), 512 * (4 + b) + C), Fn.Copy, scale=2.0)
+        diag(C - 64, C)
+        diag(128, C - 64)
+        keep(C - 64, C)
+        diag(0, 128)
+        keep(128, C - 64)
+        after(NK - 2)
+        keep(0, 128)
+        for k in range(NK - 3, NH - 1, -1):
+            after(k)
+        tt(V("eq", 0, C), V("ps", 0, C), V("fill", 0, C), Op.is_equal)
+        for k in range(NL):
+            earlier(k)
+        scan(V("nu", 0, C), V("r01", 0, C), V("eq", 0, C), 0.0, Op.mult, Op.add)
+        earlier(NH - 1)
+        tt(V("fl", C, ROW * NK, ROW), V("nu", 15, C, 16), ck, Op.add)
+        for ks in (range(NK - 1, NH - 1, -1), range(NL - 1, -1, -1)):
+            for k in ks:
+                sign(k)
+            for k in ks:
+                count(k)
+        after(NH - 1)
+        for k in range(NH - 2, NL - 1, -1):
+            earlier(k)
+            after(k)
+            total(k + 1)
+            if k == MID:
+                places(NH, NK)
+        places(MID, NH)
+        spread(NH, NK)
+        total(NL)
+        wanted(0)
+        spread(MID, NH)
+        places(NL, MID)
+        places(0, NL)
+        wanted(1)
         dcol(0)
         dcol(1)
-        spread(0, 4)
+        spread(0, MID)
+        wanted(2)
+        pl = V("pl", 0, NK)
         ts(at, pl, float(OFF + C), Op.add)
-        ts(wr, pl, float(A), Op.is_lt, ONE, Op.mult)
+        ts(wr, pl, float(A), Op.is_lt, unit[0], Op.mult)
         scan(V("eh", 0, A), hold4, V("ew", 0, A), 0.0, Op.mult, Op.add)
-        scan(V("eh", A, 2 * A), hold16, V("ew", 0, A), 0.0, Op.mult, Op.add)
-        ts(V("zl", 0, 24), V("eh", 3, A, 4), back4, Op.mult, b4, Op.add)
+        offer, zl, ML = (mx, NK, NK + 24) if t else (mine, NK + 6, NK + 6)
+        if not t:
+            scan(V("eh", A, 2 * A), hold16, V("ew", 0, A), 0.0, Op.mult, Op.add)
+        wanted(3)
         tt(mine, at, wr, Op.min)
-        ts(V("ml", NK, NK + 6), V("eh", A + 15, 2 * A, 16), back16, Op.mult, 0.25, Op.mult)
-        offer = mx if t else mine
+        ts(V("ml", zl, zl + 24), V("eh", 3, A, 4), back4, Op.mult, b4, Op.add)
         if t:
             tt(mx, mine, cF, Op.max)
-        for q, a, b in (("a", 10, 24), ("v", 0, 10)):
-            move(q, V("zt", 128 + 16 * a, 128 + 16 * b), ind(V(win, 0, 4 * C), V("zl", a, b)))
-        cp(V("ml", 0, NK), offer)
-        send(t, "am%d" % t, V("ml", 0, 28), V(lm, 0, 28))
-        landed(t, "am%d" % t, 1, [V(lm, 0, 28)])
+        else:
+            ts(V("ml", NK, NK + 6), V("eh", A + 15, 2 * A, 16), back16, Op.mult, 0.25, Op.mult)
+            cp(V("ml", 0, NK), offer)
+        for q, a in (("a", 12), ("v", 0)):
+            move(q, V("zt", 128 + 16 * a, 128 + 16 * a + 192), ind(V(win, 0, 4 * C), V("ml", zl + a, zl + a + 12)))
+        if t:
+            cp(V("ml", 0, NK), offer)
+        send(t, "am%d" % t, V("ml", 0, ML), V(lm, 0, ML))
+        landed(t, "am%d" % t, 1, [V(lm, 0, ML)])
+        tt(sp, mine, cK, Op.max)
+        ts(old, offer, 0.0, Op.is_gt, float(span), Op.mult)
         quant(V("qz", 0, 128), V("sz", 0, 128), V("zt", 0, 512))
         for b in range(4):
             mm(b, ("qw", "sw"), 128 * b, ("qz", "sz"), 0, 128)
         dcol(2)
-        tt(sp, mine, cK, Op.max)
-        tt(cn(0), cn(0), wr, Op.add)
-        ts(old, offer, 0.0, Op.is_gt, float(span), Op.mult)
-
-        def spo(b, make=False):
-            if make:
-                ts(spo(b), sp, 4.0, Op.mult, b - 4.0 * OFF, Op.add)
-            return V("so", NK * b, NK * b + NK)
-        spo(0, True)
-        spo(1, True)
         for b in range(4):
-            act(V("rl", A * b, A * b + A), V("ps", 512 * b + 32, 512 * b + 128), Fn.Relu, scale=0.03125)
-            tt(V(win, 4 * C + b, 4 * PAIR, 4), V("rl", A * b, A * b + A), V("zt", 128 + b, 512, 4), Op.add)
-        dcol(3)
+            ts(V("so", NK * b, NK * b + NK), sp, 4.0, Op.mult, b - 4.0 * OFF, Op.add)
         if t == 2:
-            digit(0, "cn", Fn.Copy)
-            for i in range(1, 4):
-                digit(i, "df", Fn.Relu)
+            tt(W(14, 48), cn(0, 48), cn(2, 48), Op.add)
+        for b in range(4):
+            s, r = V("ps", 512 * b + 32, 512 * b + 128), V("rl", A * b, A * b + A)
+            if b:
+                act(r, s, Fn.Relu, scale=0.03125)
+            else:
+                ts(r, s, 0.0, Op.max, 0.03125, Op.mult)
+            tt(V(win, 4 * C + b, 4 * PAIR, 4), r, V("zt", 128 + b, 512, 4), Op.add)
+        dcol(3)
         quant(V("qh", 0, 128), V("sh", 0, 128), V(win, 4 * PAIR - 512, 4 * PAIR))
         send(t, "ah%d" % t, V("qh", 32, 128), V(lq, LH, LH + A))
         send(t, "ah%d" % t, V("sh", 32, 128), V(ls, LH, LH + A))
-        them, ep = V(lm, 0, NK), V(lm, NK, NK + 6)
+        them, ep = V(lm, 0, NK), V(lm, NK, ML)
 
-        def half(b, q):
-            move(q, V("xh", C * b, C * b + C), ind(V(win, 0, 4 * PAIR), spo(b)), 0.5)
+        def xh(b, k0=0, k1=NK):
+            return V("xh", 64 * k0 + b, 64 * k1, 4) if t else V("xh", C * b + 16 * k0, C * b + 16 * k1)
+
+        def half(b, q, k0=0, k1=NK):
+            move(q, xh(b, k0, k1), ind(V(win, 0, 4 * PAIR), V("so", NK * b + k0, NK * b + k1)), 0.5)
 
         def mean(b):
-            tt(V(win, 8 * PAIR + b, 8 * PAIR + 4 * C, 4), V("ps", 512 * (4 + b), 512 * (4 + b) + C), V("xh", C * b, C * b + C), Op.add)
-
-        def owns(b):
-            act(V("oh", A * b, A * b + A), ind(V("xh", C * b, C * b + C), ep), Fn.Copy)
+            tt(V(win, 8 * PAIR + b, 8 * PAIR + 4 * C, 4), V("ps", 512 * (4 + b), 512 * (4 + b) + C), xh(b), Op.add)
 
         def offsets():
             for b in range(4):
                 ts(V("fo", NK * b, NK * b + NK), t5, 4.0, Op.mult, b - 4.0 * OFF, Op.add)
-        half(0, "a")
-        spo(2, True)
-        spo(3, True)
         if t == 0:
             iota(V("any", 0, 16), [[0, 16]], 0, 0)
             iota(V("any", 16, 3 * PAIR), [[0, 3 * PAIR - 16]], 1, 0)
-            half(1, "a")
-            half(2, "v")
+            half(0, "a")
             half(3, "v")
+            half(1, "a")
+            fillc(V("nil", 0, 512), 0.0)
+            ts(cw2, cK, 2.0, Op.mult, -2.0 * OFF - C, Op.add)
+            half(2, "a")
             quant(V("qe", 0, 512), V("se", 0, 512), et)
+            quant(V("lq0", 0, 128), V("ls0", 0, 128), V("nil", 0, 512))
             ts(mf, them, float(span), Op.add)
-            ts(cn(1), them, 0.0, Op.is_gt, ONE, Op.mult)
-            tt(mf, mf, old, Op.add)
-            for b in range(4):
-                owns(b)
             quant(V("qv", 0, 128), V("sv", 0, 128), V("vt", 0, 512))
+            tt(mf, mf, old, Op.add)
+            for b in (1, 3, 0, 2):
+                act(V("oh", b, 4 * A, 4), ind(xh(b), ep), Fn.Copy)
             tt(t5, mf, sp, Op.max)
             offsets()
         else:
-            half(1, "a")
-            half(3, "v")
             act(V("row", 0, C), ind(V("any", 0, 3 * PAIR), them), Fn.Copy)
-            mean(0)
-            half(2, "v")
+            half(0, "a")
+            half(3, "v")
             ts(mf, them, float(span), Op.add)
-            if t == 1:
-                ts(wp, them, float(OFF + C), Op.is_ge, ONE, Op.mult)
-                steps = [lambda: None,
-                         lambda: tt(wp, wp, V(lc, 0, NK), Op.add),
-                         lambda: tt(cn(2), V(lc, 24, 24 + NK), recv, Op.min),
-                         lambda: tt(cn(3), wp, recv, Op.min)]
-            else:
-                ts(V("pk", 24, 24 + NK), them, float(OFF + C), Op.is_ge, 16.0, Op.mult)
-                steps = [lambda: tt(W(14, 96), V("pk", 0, 96), V("pk", 96, 192), Op.add),
-                         lambda: tt(W(14, 48), W(14, 48), W(16, 48), Op.add),
-                         lambda: tt(W(15), W(15), recv, Op.min),
-                         lambda: tt(W(14), W(14), W(15), Op.add)]
-            tt(mf, mf, old, Op.add)
-            steps[0]()
             scan(V("row", C, 2 * C), V("row", 0, C), V("row", 0, C), 0.0, Op.add, Op.max)
             act(V("row", 2 * C, 3 * C), V("row", C, 2 * C), Fn.Sign, bias=K + 0.5, scale=-1.0, acc=V("acc", 0, 1))
-            for b in (0, 3, 1, 2):
-                owns(b)
-            steps[1]()
+            half(1, "a")
+            tt(mf, mf, old, Op.add)
+            if t == 2:
+                tt(W(14), W(14), W(15), Op.add)
             mean(3)
+            half(2, "v", 0, 10)
+            half(2, "a", 10, NK)
+            act(V("oh", 0, 4 * A), ind(V("xh", 0, 4 * C), ep), Fn.Copy)
             ts(cap, cw2, V("acc", 0, 1), Op.is_ge, -ONE, Op.mult)
-            mean(1)
+            mean(0)
             tt(mf, mf, cap, Op.add)
-            mean(2)
+            if t == 2:
+                tt(W(14), W(14), wr, Op.add)
+            mean(1)
             tt(t5, mf, sp, Op.max)
-            ts(recv, mf, float(OFF), Op.is_gt, 4 * ONE, Op.mult)
+            mean(2)
             offsets()
-            steps[2]()
-            steps[3]()
-        if t + 1 < R:
-            send(t + 1, "ac%d" % (t + 1), cn(0, 48 * t + 48), V("lc%d" % (t + 1), 0, 48 * t + 48))
-            landed(t + 1, "ac%d" % (t + 1), 1, [V("lc%d" % (t + 1), 0, 48 * t + 48)])
+        if t == 2:
+            act(V("pk", 24, 96), V("df", 24, 96), Fn.Relu, scale=-1.0)
+            ts(V("pk", 0, 24), V(lm, 0, 24), float(OFF + C), Op.is_ge, unit[2], Op.mult)
         landed(t, "ah%d" % t, 2, [V(lq, LH, LH + A), V(ls, LH, LH + A)])
-        for b in range(4):
-            mm(b, QE, 128 * b, (lq, ls), LH - 32, 128)
-        for i, b in enumerate((0, 1, 2, 3, 1, 0, 3, 2)):
-            d = V("ps", 512 * b + 32, 512 * b + 128)
-            if i % 2:
-                tt(V(win, DH + 4 * span + b, DH + 4 * (span + A), 4), d, V("oh", A * b, A * b + A), Op.add)
+        for bank in (1, 4, 3, 6, 0, 2):
+            mm(bank, QE, 128 * (bank % 4), (lq, ls), LH - 32, 128)
+        for q, b in (("m", 1), ("v", 1), ("a", 0), ("m", 3), ("v", 3), ("a", 2), ("m", 0), ("m", 2)):
+            bank = b + 4 * (q == "a")
+            d = V("ps", 512 * bank + 32, 512 * bank + 128)
+            if q == "m":
+                tt(V(win, DH + 4 * span + b, DH + 4 * (span + A), 4), d, V("oh", b, 4 * A, 4), Op.add)
             else:
-                act(V(win, DH + b, DH + 4 * A, 4), d, Fn.Copy, scale=2.0)
+                move(q, V(win, DH + b, DH + 4 * A, 4), d, 2.0)
         if t + 1 < R:
             for b in range(4):
                 move("v" if b < 2 else "a", V(nxt, b, 4 * C, 4), ind(whole, V("fo", NK * b, NK * b + NK)))
@@ -493,7 +497,7 @@ def rank_program(g, core, T, topo):
 
     def gather(i, b):
         k0, k1 = runs[i]
-        move("v" if b < 2 else "a", V(nxt, 64 * k0 + b, 64 * k1, 4), ind(whole, V("fo", NK * b + k0, NK * b + k1)))
+        move("v" if b < 2 - i else "a", V(nxt, 64 * k0 + b, 64 * k1, 4), ind(whole, V("fo", NK * b + k0, NK * b + k1)))
 
     def pack(i):
         a, z = 16 * runs[i][0], 16 * runs[i][1]
@@ -501,20 +505,31 @@ def rank_program(g, core, T, topo):
         mm(i, ("qv", "sv"), 0, QX, a, z - a)
         dma("s", T.oc[:, 4 * a:4 * z], T.qx[:, a:z].bitcast(dt.uint8), [V("qx", a, z)], [])
 
-    def result(i, q):
+    def result(i):
         a, z = 16 * runs[i][0], 16 * runs[i][1]
-        move(q, V("yt", a, z), V("ps", 512 * i, 512 * i + z - a))
-        dma("a", T.y[:, a:z], T.yt[:, a:z], [V("yt", a, z)], [])
-    cp(V("wu", 0, NK), W(14))
-    for i, b in ((0, 0), (0, 2), (0, 1), (0, 3), (1, 0), (1, 2), (1, 3)):
-        gather(i, b)
+        cp(V("yt", a, z), V("ps", 512 * i, 512 * i + z - a))
+        dma("s", T.y[:, a:z], T.yt[:, a:z], [V("yt", a, z)], [])
+
+    def scales(q, ks):
+        for k in ks:
+            dma(q, T.osc[4 * k:4 * k + 4, :], T.sx[32 * k:32 * k + 4, :], [V("sx", 0, C)], [])
+    tt(W(16, 48), V("pk", 0, 48), V("pk", 48, 96), Op.add)
+    ts(recv, mf, float(OFF), Op.is_gt, 256 * ONE, Op.mult)
+    for b in (0, 2, 3):
+        gather(0, b)
+    tt(W(16), W(16), W(17), Op.add)
+    gather(0, 1)
+    tt(W(16), W(16), recv, Op.min)
     pack(0)
-    gather(1, 1)
+    tt(W(14), W(14), W(16), Op.add)
+    for b in range(4):
+        gather(1, b)
+    ts(V("wu", 0, NK), W(14), 1 / ONE, Op.mult)
     pack(1)
-    result(0, "a")
-    for k in range(4):
-        dma("s", T.osc[4 * k:4 * k + 4, :], T.sx[32 * k:32 * k + 4, :], [V("sx", 0, C)], [])
-    cp(V("ovr", 0, C), ind(V("tab", 0, 256), V("wu", 0, NK)))
-    dma("s", T.ov[:], T.ovr[0:128:16, :], [V("ovr", 0, C)], [])
-    result(1, "a")
+    act(V("ovr", 0, C), ind(V("tab", 0, 256), V("wu", 0, NK)), Fn.Copy)
+    scales("s", (0, 1))
+    result(0)
+    scales("a", (2, 3))
+    result(1)
+    dma("a", T.ov[:], T.ovr[0:128:16, :], [V("ovr", 0, C)], [])
     emit()

from concourse.bass import DstId, RemoteDMATransfer
from concourse.mybir import dt, AluOpType, ActivationFunctionType

C, A, K, R = 352, 96, 160, 3
STEP = [1, 6, 7]
NK = C // 16
NL, NH = 4, 16
MID = NL + 2
HALF = C // 2
ROW = C + 2
BIG = 2.0 ** 96
LOW = 128.0
PAIR = C + A
OFF = 2 * PAIR
ONE = 4096.0
JUMP = 65536.0
F8, U8, BF, F32, I32, U16 = "float8_e4m3fn_x4", "uint8", "bfloat16", "float32", "int32", "uint16"

SCRATCH = {
    "ps": ("psum", [128, 4096], F32),
    "w0": ("sbuf", [128, 4 * (PAIR + 2 * A)], BF), "w1": ("sbuf", [128, 12 * PAIR], BF), "w2": ("sbuf", [128, 12 * PAIR], BF),
    "w3": ("sbuf", [128, 4 * C], BF), "xh": ("sbuf", [128, 4 * C], BF), "oh": ("sbuf", [128, 4 * A], BF),
    "zt": ("sbuf", [128, 512], BF), "rl": ("sbuf", [128, 4 * A], F32), "yt": ("sbuf", [128, C], F32), "nil": ("sbuf", [128, 512], BF),
    "ut": ("sbuf", [128, 512], BF), "vt": ("sbuf", [128, 512], BF), "et": ("sbuf", [128, 2048], BF),
    "qu": ("sbuf", [128, 128], F8), "su": ("sbuf", [128, 128], U8), "qur": ("sbuf", [128, 128], F8), "sur": ("sbuf", [128, 128], U8),
    "qv": ("sbuf", [128, 128], F8), "sv": ("sbuf", [128, 128], U8), "qw": ("sbuf", [128, 512], F8), "sw": ("sbuf", [128, 512], U8),
    "qe": ("sbuf", [128, 512], F8), "se": ("sbuf", [128, 512], U8), "qx": ("sbuf", [128, C], F8), "sx": ("sbuf", [128, C], U8),
    "qz": ("sbuf", [128, 128], F8), "sz": ("sbuf", [128, 128], U8), "qh": ("sbuf", [128, 128], F8), "sh": ("sbuf", [128, 128], U8),
    "pi": ("sbuf", [128, 8], I32), "pf": ("sbuf", [128, 8], F32), "k16": ("sbuf", [128, NK], F32), "uo": ("sbuf", [128, 8], U16),
    "jt": ("sbuf", [128, C], F32), "md": ("sbuf", [128, C], F32), "rs": ("sbuf", [128, C], F32), "r01": ("sbuf", [128, C], BF),
    "i4": ("sbuf", [128, C], F32), "j4": ("sbuf", [128, A], F32), "hold": ("sbuf", [128, 2 * A], F32), "col": ("sbuf", [128, 72], F32),
    "tab": ("sbuf", [128, 256], F32), "any": ("sbuf", [128, 3 * PAIR], BF),
    "d1": ("sbuf", [128, C], F32), "fill": ("sbuf", [128, C], F32), "eq": ("sbuf", [128, C], BF), "nu": ("sbuf", [128, C], BF),
    "fl": ("sbuf", [128, ROW * NK], BF), "sc": ("sbuf", [128, HALF * NK], BF), "gl": ("sbuf", [128, NK], F32),
    "pl": ("sbuf", [128, NK], U16), "ew": ("sbuf", [128, C], F32), "eh": ("sbuf", [128, 2 * A], F32),
    "ml": ("sbuf", [128, 52], U16), "so": ("sbuf", [128, 4 * NK], U16),
    "cn": ("sbuf", [128, 96], BF), "df": ("sbuf", [128, 96], F32), "w": ("sbuf", [128, 24 * 18], F32), "wu": ("sbuf", [128, NK], U16),
    "fo": ("sbuf", [128, 4 * NK], U16), "row": ("sbuf", [128, 3 * C], BF), "acc": ("sbuf", [128, 2], F32),
    "pk": ("sbuf", [128, 96], F32), "ovr": ("sbuf", [128, C], F32),
}
for _t in range(R):
    SCRATCH["lq%d" % _t] = ("sbuf", [128, (C if _t else 128) + A], F8)
    SCRATCH["ls%d" % _t] = ("sbuf", [128, (C if _t else 128) + A], U8)
    SCRATCH["lm%d" % _t] = ("sbuf", [128, 46], U16)
    if _t:
        SCRATCH["lc%d" % _t] = ("sbuf", [128, 48 * _t], BF)
SEMAPHORES = ["cv", "ca", "ct", "cg"] + ["a%s%d" % (k, t) for k in "hmxc" for t in range(R) if t or k in "hm"] + ["d%d" % i for i in range(44)]


def make_plan(g, T):
    ops, free = [], ["d%d" % i for i in range(44)]

    def view(name, a, b, step=1):
        ap = T[name][:, a:b] if step == 1 else T[name][:, a:b:step]
        if name == "ps":
            a, b, step = a // 512 * 512, (b + 511) // 512 * 512, 1
        return (ap, name, set(range(a, b, step)))

    def note(q, fn, reads, writes, kind="c", sem=None, n=0):
        if kind in "dr":
            sem = free.pop(0)
        ops.append({"q": q, "fn": fn, "r": reads, "w": writes, "kind": kind, "sem": sem, "n": n, "deps": [], "used": False})

    def emit():
        eng = {"v": g.vector, "a": g.scalar, "t": g.tensor, "g": g, "s": g.sync}
        seen = {}
        clock = {q: {} for q in eng}
        for i, o in enumerate(ops):
            need = set()
            for (ap, name, cols), wr in [(x, False) for x in o["r"]] + [(x, True) for x in o["w"]]:
                for j, c2, w2 in seen.get(name, []):
                    if (wr or w2 or (name == "ps" and ops[j]["q"] != o["q"])) and not cols.isdisjoint(c2):
                        need.add(j)
            for (ap, name, cols), wr in [(x, False) for x in o["r"]] + [(x, True) for x in o["w"]]:
                seen.setdefault(name, []).append((i, cols, wr))
            if o["kind"] == "x":
                o["clock"] = {o["sem"]: i}
                continue
            ck = clock[o["q"]]
            for j in sorted(need, reverse=True):
                key = ops[j]["sem"] or ops[j]["q"]
                if ck.get(key, -1) < j:
                    o["deps"].append(j)
                    ops[j]["used"] = True
                    for k2, v2 in ops[j]["clock"].items():
                        ck[k2] = max(ck.get(k2, -1), v2)
            o["clock"] = dict(ck)
            o["clock"][o["sem"] or o["q"]] = i
        count = {q: 0 for q in eng}
        for o in ops:
            e = eng.get(o["q"])
            for j in o["deps"]:
                e.wait_ge(T.sem[ops[j]["sem"] or "c" + ops[j]["q"]], ops[j]["n"])
            if o["kind"] == "c":
                ins = o["fn"](e)
                if o["used"]:
                    count[o["q"]] += 1
                    o["n"] = count[o["q"]]
                    ins.then_inc(T.sem["c" + o["q"]], 1)
            elif o["kind"] == "d":
                o["fn"](e).then_inc(T.sem[o["sem"]], 16)
            elif o["kind"] == "r":
                o["fn"](T.sem[o["sem"]])
        for o in ops:
            if o["kind"] != "c" and not o["used"]:
                eng[o["q"] if o["q"] in eng else "g"].wait_ge(T.sem[o["sem"]], o["n"])
    return view, note, emit


def rank_program(g, core, T, topo):
    rank = T.rank_of(core)
    if rank is None:
        return
    V, note, emit = make_plan(g, T)
    Op, Fn = AluOpType, ActivationFunctionType

    def ind(win, off):
        return (win[0].indirect(off[0]), win[1], win[2], off)

    def rd(*xs):
        out = []
        for x in xs:
            if isinstance(x, tuple):
                out.append(x[:3])
                out.extend(x[3:])
        return out

    def ap(x):
        return x[0] if isinstance(x, tuple) else x

    def tt(out, a, b, op):
        note("v", lambda e: e.tensor_tensor(out[0], a[0], b[0], op), rd(a, b), [out])

    def ts(out, a, s1, op0, s2=None, op1=None):
        if op1 is None:
            note("v", lambda e: e.tensor_scalar(out[0], a[0], ap(s1), None, op0), rd(a, s1), [out])
        else:
            note("v", lambda e: e.tensor_scalar(out[0], a[0], ap(s1), ap(s2), op0, op1), rd(a, s1, s2), [out])

    def cp(out, a):
        note("v", lambda e: e.tensor_copy(out[0], a[0]), rd(a) + list(out[3:]), [out[:3]])

    def scan(out, a, b, init, op0, op1):
        note("v", lambda e: e.tensor_tensor_scan(out[0], a[0], b[0], ap(init), op0, op1), rd(a, b, init), [out])

    def fillc(out, c):
        note("v", lambda e: e.memset(out[0], c), [], [out])

    def act(out, a, f, bias=None, scale=None, acc=None):
        kw = {k: ap(x) for k, x in (("bias", bias), ("scale", scale), ("accum_out", acc)) if x is not None}
        note("a", lambda e: e.activation(out[0], a[0], f, **kw), rd(a, bias), [out] + rd(acc))

    def move(q, out, a, scale=None):
        if q == "a":
            act(out, a, Fn.Copy, scale=scale)
        elif scale is None:
            cp(out, a)
        else:
            ts(out, a, scale, Op.mult)

    def quant(q, s, a):
        note("v", lambda e: e.quantize_mx(q[0], s[0], a[0]), [a], [q, s])

    def mm(bank, w, c0, x, a, n):
        out, lq, lsc, rq, rsc = V("ps", 512 * bank, 512 * bank + n), V(w[0], c0, c0 + 128), V(w[1], c0, c0 + 128), V(x[0], a, a + n), V(x[1], a, a + n)
        note("t", lambda e: e.matmul_mx(out[0], lq[0], lsc[0], rq[0], rsc[0], True, True), [lq, lsc, rq, rsc], [out])

    def iota(out, pattern, base, cm, small=True):
        if small:
            note("g", lambda e: e.iota(out[0], pattern, base, cm, allow_small_or_imprecise_dtypes=True), [], [out])
        else:
            note("g", lambda e: e.iota(out[0], pattern, base, cm), [], [out])

    def dma(q, out, in_, reads, writes):
        note(q, lambda e: e.dma_start(out, in_), reads, writes, kind="d", n=16)

    def u8(x):
        return x[0].bitcast(dt.uint8) if SCRATCH[x[1]][2] == F8 else x[0]

    def send(t, sem, src, dst):
        to = T.cores[rank ^ STEP[t]]
        rid, pid = topo.addr(to, core)
        note("g", lambda ls: g.remote_dma(u8(dst), u8(src), T.sem[sem], ls, pid, rid, topo.mask(core, to)), [src], [], kind="r", n=len(topo.engines(core, to)))

    def landed(t, sem, calls, views):
        note("x", None, [], views, kind="x", sem=sem, n=calls * len(topo.engines(T.cores[rank ^ STEP[t]], core)))

    def W(i, n=NK):
        return V("w", 24 * i, 24 * i + n)

    def cn(i, n=NK):
        return V("cn", 24 * i, 24 * i + n)

    rel = [rank, rank ^ STEP[0], rank ^ STEP[2], rank ^ STEP[1]]
    four = sorted(rel)
    unit = [ONE * 4 ** four.index(r) for r in rel]

    dma("s", T.ut[:], T.u[:], [], [V("ut", 0, 512)])
    dma("a", T.w0[:, 0:2 * C], T.x[:, 0:2 * C], [], [V("w0", 0, 2 * C)])
    dma("s", T.w0[:, 2 * C:4 * C], T.x[:, 2 * C:4 * C], [], [V("w0", 2 * C, 4 * C)])
    later = [V("w0", 0, 4 * C)]
    dma("s", T.qw[:].bitcast(dt.uint8), T.wc[:], later, [V("qw", 0, 512)])
    dma("s", T.sw[:], T.ws[:], [], [V("sw", 0, 512)])
    dma("s", T.vt[:], T.v[:], [], [V("vt", 0, 512)])
    fillc(V("et", 0, 2048), 0.0)
    iota(V("pi", 0, 2), [[0, 2]], 0, 1, small=False)
    iota(V("k16", 0, NK), [[16, NK]], 0, 0)
    iota(V("jt", 0, C), [[0, NK], [1, 16]], 0, 0)
    iota(V("j4", 0, A), [[0, A // 4], [1, 4]], 0, 0)
    iota(V("i4", 0, C), [[4, C]], 0, 0)
    et = V("et", 0, 2048)
    note("g", lambda e: e.affine_select(et[0], et[0], [[-1, 4], [1, 512]], Op.not_equal, 0.5, 0, -4), [et], [et])
    q16, q4, b4, back16, back4 = [V("pf", i, i + 1) for i in (0, 2, 4, 6, 7)]
    cK, cw2, ck = [V("col", 24 * i, 24 * i + NK) for i in range(3)]
    cp(V("uo", 0, 8), V("k16", 0, 8))
    ts(V("pi", 2, 4), V("pi", 0, 2), 15, Op.bitwise_and)
    ts(V("pi", 4, 6), V("pi", 0, 2), 2, Op.logical_shift_right, 3, Op.bitwise_and)
    ts(V("pi", 6, 8), V("pi", 0, 2), 3, Op.bitwise_and)
    fillc(V("col", 48, 48 + NL), -16.0)
    cp(V("pf", 0, 6), V("pi", 2, 8))
    fillc(V("col", 48 + NL, 48 + NH), LOW)
    ts(V("md", 0, C), V("jt", 0, C), q16, Op.is_equal, 2 * BIG, Op.mult)
    fillc(V("col", 48 + NH, 48 + NK), 0.0)
    ts(back16, q16, 15.0, Op.is_equal, 1 / JUMP, Op.max)
    ts(back4, q4, 3.0, Op.is_equal, 1 / JUMP, Op.max)
    ts(cK, V("k16", 0, NK), q16, Op.add, float(OFF), Op.add)
    fillc(V("zt", 0, 128), 0.0)
    fillc(V("cn", 0, 96), 0.0)
    act(V("r01", 0, C), V("jt", 0, C), Fn.Sign)
    act(V("rs", 0, C), V("r01", 0, C), Fn.Identity, bias=-BIG, scale=2 * BIG)
    act(V("md", 0, C), V("md", 0, C), Fn.Identity, bias=-BIG)
    hold16, hold4, hold = V("hold", 0, A), V("hold", A, 2 * A), V("hold", 0, 2 * A)
    act(hold16, V("jt", 0, A), Fn.Abs, bias=q16, scale=-1.0)
    act(hold4, V("j4", 0, A), Fn.Abs, bias=q4, scale=-1.0)
    quant(V("qu", 0, 128), V("su", 0, 128), V("ut", 0, 512))
    uo = V("uo", 0, 8)
    note("v", lambda e: e.tensor_copy(T.qur[:, 0:128].bitcast(dt.uint32), T.qu[:, 0:128].bitcast(dt.uint32).indirect(uo[0])), [V("qu", 0, 128), uo], [V("qur", 0, 128)])
    act(V("sur", 0, 128), ind(V("su", 0, 128), uo), Fn.Copy)
    act(hold, hold, Fn.Relu, bias=2.0, scale=-1.0)
    act(hold, hold, Fn.Abs, bias=-3.0, scale=4.0)
    act(hold, hold, Fn.Relu, bias=1.5 * JUMP - 0.5, scale=0.5 - JUMP / 2)

    QX, QE = ("qx", "sx"), ("qe", "se")
    at, wr, mine, mx, sp, old, cF, mf, cap, recv, wp, t5 = [W(i) for i in range(12)]
    for t in range(R):
        win, nxt = "w%d" % t, "w%d" % (t + 1)
        span = PAIR if t else A
        DH = 4 * (PAIR + span - A)
        whole = V(win, 0, DH + 4 * (span + A))
        lq, ls, lm, lc = "lq%d" % t, "ls%d" % t, "lm%d" % t, "lc%d" % t
        LH = C if t else 128
        if t == 0:
            for a in (0, HALF):
                quant(V("qx", a, a + HALF), V("sx", a, a + HALF), V(win, 4 * a, 4 * a + 2 * C))
        else:
            quant(V("qx", 0, C), V("sx", 0, C), V(win, 0, 4 * C))
        mm(0, ("qur", "sur"), 0, QX, 0, C)
        mm(1, ("qur", "sur"), 0, QX, 0, C)
        if t:
            tt(cn(0), cn(0), wr, Op.add)
        if t == 1:
            ts(cn(1), them, 0.0, Op.is_gt, unit[1], Op.mult)
        if t == 2:
            ts(wp, them, float(OFF + C), Op.is_ge, unit[3], Op.mult)
            ts(recv, mf, float(OFF), Op.is_gt, 256 * ONE, Op.mult)
            tt(wp, wp, V("lc1", 0, NK), Op.add)
            tt(cn(2), V("lc1", 24, 24 + NK), recv, Op.min)
            tt(cn(3), wp, recv, Op.min)
        if t:
            CL = 46 if t == 1 else 96
            send(t, "ax%d" % t, V("qx", 0, C), V(lq, 0, C))
            send(t, "ac%d" % t, cn(0, CL), V(lc, 0, CL))
            send(t, "ax%d" % t, V("sx", 0, C), V(ls, 0, C))
            landed(t, "ac%d" % t, 1, [V(lc, 0, CL)])
            landed(t, "ax%d" % t, 2, [V(lq, 0, C), V(ls, 0, C)])
            for b in range(4):
                mm(4 + b, QE, 128 * b, (lq, ls), 0, C)
        if t == 1:
            tt(W(12), cn(0), cn(1), Op.max)
            for d3 in range(4):
                iota(V("tab", 64 * d3, 64 * d3 + 64), [[4 ** four[2], 4], [4 ** four[1], 4], [4 ** four[0], 4]], d3 * 4 ** four[3], 0)

        def diag(a, b):
            tt(V("d1", a, b), V("ps", a, b), V("md", a, b), Op.min)

        def keep(a, b):
            scan(V("fill", a, b), V("rs", a, b), V("d1", a, b), -BIG, Op.min, Op.max)

        def own(k):
            return V("fill", 16 * k + 15, 16 * k + 16)

        def fl(k, a, b):
            return V("fl", ROW * k + a, ROW * k + b)

        def earlier(k):
            ts(fl(k, 0, 16 * k + 16), V("ps", 0, 16 * k + 16), own(k), Op.is_ge, -1.0, Op.mult)

        def after(k):
            e = 16 * k + 16
            if k < NH:
                ts(fl(k, e, C), V("ps", e, C), own(k), Op.is_gt, -1.0, Op.mult)
            else:
                ts(fl(k, e, C), V("ps", e, C), own(k), Op.is_le)

        def total(k):
            scan(V("sc", HALF * k, HALF * k + HALF), fl(k, 0, HALF), fl(k, HALF, C), fl(k, C, C + 1), Op.add, Op.add)

        def sign(k):
            a, b = (16 * k + 16, C) if k < NL else (0, 16 * k + 16)
            act(fl(k, a, b), V("ps", 512 + a, 512 + b), Fn.Sign, bias=own(k), scale=-1.0)

        def count(k):
            act(fl(k, 0, C + 1), fl(k, 0, C + 1), Fn.Relu, scale=-1.0 if k < NL else 1.0, acc=V("gl", k, k + 1))

        def places(a, b):
            if a >= NH:
                ts(V("pl", a, b), V("gl", a, b), -1.0, Op.mult, float(C), Op.add)
            elif a >= NL:
                ts(V("pl", a, b), V("sc", HALF * a + HALF - 1, HALF * b, HALF), -1.0, Op.mult, LOW, Op.add)
            else:
                ts(V("pl", a, b), V("gl", a, b), -16.0, Op.add)

        def spread(a, b):
            cp(ind(V("ew", 0, C), V("pl", a, b)), V("i4", 16 * a, 16 * b))

        def wanted(i):
            if t == 1 and i == 0:
                tt(cF, W(12), cK, Op.min)
            if t == 2 and i == 0:
                tt(V("df", 0, 48), cn(0, 48), V(lc, 48, 96), Op.subtract)
                tt(V("df", 48, 96), cn(2, 48), V(lc, 0, 48), Op.subtract)
            if t == 2 and i == 1:
                tt(W(12), V("df", 0, NK), V("df", 24, 24 + NK), Op.max)
                tt(W(13), V("df", 72, 72 + NK), cK, Op.min)
            if t == 2 and i == 2:
                tt(W(12), W(12), cK, Op.min)
            if t == 2 and i == 3:
                tt(cF, W(12), W(13), Op.max)

        def dcol(b):
            if t:
                act(V(win, 4 * PAIR + b, DH, 4), V("ps", 512 * (4 + b), 512 * (4 + b) + C), Fn.Copy, scale=2.0)
        diag(C - 64, C)
        diag(128, C - 64)
        keep(C - 64, C)
        diag(0, 128)
        keep(128, C - 64)
        after(NK - 2)
        keep(0, 128)
        for k in range(NK - 3, NH - 1, -1):
            after(k)
        tt(V("eq", 0, C), V("ps", 0, C), V("fill", 0, C), Op.is_equal)
        for k in range(NL):
            earlier(k)
        scan(V("nu", 0, C), V("r01", 0, C), V("eq", 0, C), 0.0, Op.mult, Op.add)
        earlier(NH - 1)
        tt(V("fl", C, ROW * NK, ROW), V("nu", 15, C, 16), ck, Op.add)
        for ks in (range(NK - 1, NH - 1, -1), range(NL - 1, -1, -1)):
            for k in ks:
                sign(k)
            for k in ks:
                count(k)
        after(NH - 1)
        for k in range(NH - 2, NL - 1, -1):
            earlier(k)
            after(k)
            total(k + 1)
            if k == MID:
                places(NH, NK)
        places(MID, NH)
        spread(NH, NK)
        total(NL)
        wanted(0)
        spread(MID, NH)
        places(NL, MID)
        places(0, NL)
        wanted(1)
        dcol(0)
        dcol(1)
        spread(0, MID)
        wanted(2)
        pl = V("pl", 0, NK)
        ts(at, pl, float(OFF + C), Op.add)
        ts(wr, pl, float(A), Op.is_lt, unit[0], Op.mult)
        scan(V("eh", 0, A), hold4, V("ew", 0, A), 0.0, Op.mult, Op.add)
        offer, zl, ML = (mx, NK, NK + 24) if t else (mine, NK + 6, NK + 6)
        if not t:
            scan(V("eh", A, 2 * A), hold16, V("ew", 0, A), 0.0, Op.mult, Op.add)
        wanted(3)
        tt(mine, at, wr, Op.min)
        ts(V("ml", zl, zl + 24), V("eh", 3, A, 4), back4, Op.mult, b4, Op.add)
        if t:
            tt(mx, mine, cF, Op.max)
        else:
            ts(V("ml", NK, NK + 6), V("eh", A + 15, 2 * A, 16), back16, Op.mult, 0.25, Op.mult)
            cp(V("ml", 0, NK), offer)
        for q, a in (("a", 12), ("v", 0)):
            move(q, V("zt", 128 + 16 * a, 128 + 16 * a + 192), ind(V(win, 0, 4 * C), V("ml", zl + a, zl + a + 12)))
        if t:
            cp(V("ml", 0, NK), offer)
        send(t, "am%d" % t, V("ml", 0, ML), V(lm, 0, ML))
        landed(t, "am%d" % t, 1, [V(lm, 0, ML)])
        tt(sp, mine, cK, Op.max)
        ts(old, offer, 0.0, Op.is_gt, float(span), Op.mult)
        quant(V("qz", 0, 128), V("sz", 0, 128), V("zt", 0, 512))
        for b in range(4):
            mm(b, ("qw", "sw"), 128 * b, ("qz", "sz"), 0, 128)
        dcol(2)
        for b in range(4):
            ts(V("so", NK * b, NK * b + NK), sp, 4.0, Op.mult, b - 4.0 * OFF, Op.add)
        if t == 2:
            tt(W(14, 48), cn(0, 48), cn(2, 48), Op.add)
        for b in range(4):
            s, r = V("ps", 512 * b + 32, 512 * b + 128), V("rl", A * b, A * b + A)
            if b:
                act(r, s, Fn.Relu, scale=0.03125)
            else:
                ts(r, s, 0.0, Op.max, 0.03125, Op.mult)
            tt(V(win, 4 * C + b, 4 * PAIR, 4), r, V("zt", 128 + b, 512, 4), Op.add)
        dcol(3)
        quant(V("qh", 0, 128), V("sh", 0, 128), V(win, 4 * PAIR - 512, 4 * PAIR))
        send(t, "ah%d" % t, V("qh", 32, 128), V(lq, LH, LH + A))
        send(t, "ah%d" % t, V("sh", 32, 128), V(ls, LH, LH + A))
        them, ep = V(lm, 0, NK), V(lm, NK, ML)

        def xh(b, k0=0, k1=NK):
            return V("xh", 64 * k0 + b, 64 * k1, 4) if t else V("xh", C * b + 16 * k0, C * b + 16 * k1)

        def half(b, q, k0=0, k1=NK):
            move(q, xh(b, k0, k1), ind(V(win, 0, 4 * PAIR), V("so", NK * b + k0, NK * b + k1)), 0.5)

        def mean(b):
            tt(V(win, 8 * PAIR + b, 8 * PAIR + 4 * C, 4), V("ps", 512 * (4 + b), 512 * (4 + b) + C), xh(b), Op.add)

        def offsets():
            for b in range(4):
                ts(V("fo", NK * b, NK * b + NK), t5, 4.0, Op.mult, b - 4.0 * OFF, Op.add)
        if t == 0:
            iota(V("any", 0, 16), [[0, 16]], 0, 0)
            iota(V("any", 16, 3 * PAIR), [[0, 3 * PAIR - 16]], 1, 0)
            half(0, "a")
            half(3, "v")
            half(1, "a")
            fillc(V("nil", 0, 512), 0.0)
            ts(cw2, cK, 2.0, Op.mult, -2.0 * OFF - C, Op.add)
            half(2, "a")
            quant(V("qe", 0, 512), V("se", 0, 512), et)
            quant(V("lq0", 0, 128), V("ls0", 0, 128), V("nil", 0, 512))
            ts(mf, them, float(span), Op.add)
            quant(V("qv", 0, 128), V("sv", 0, 128), V("vt", 0, 512))
            tt(mf, mf, old, Op.add)
            for b in (1, 3, 0, 2):
                act(V("oh", b, 4 * A, 4), ind(xh(b), ep), Fn.Copy)
            tt(t5, mf, sp, Op.max)
            offsets()
        else:
            act(V("row", 0, C), ind(V("any", 0, 3 * PAIR), them), Fn.Copy)
            half(0, "a")
            half(3, "v")
            ts(mf, them, float(span), Op.add)
            scan(V("row", C, 2 * C), V("row", 0, C), V("row", 0, C), 0.0, Op.add, Op.max)
            act(V("row", 2 * C, 3 * C), V("row", C, 2 * C), Fn.Sign, bias=K + 0.5, scale=-1.0, acc=V("acc", 0, 1))
            half(1, "a")
            tt(mf, mf, old, Op.add)
            if t == 2:
                tt(W(14), W(14), W(15), Op.add)
            mean(3)
            half(2, "v", 0, 10)
            half(2, "a", 10, NK)
            act(V("oh", 0, 4 * A), ind(V("xh", 0, 4 * C), ep), Fn.Copy)
            ts(cap, cw2, V("acc", 0, 1), Op.is_ge, -ONE, Op.mult)
            mean(0)
            tt(mf, mf, cap, Op.add)
            if t == 2:
                tt(W(14), W(14), wr, Op.add)
            mean(1)
            tt(t5, mf, sp, Op.max)
            mean(2)
            offsets()
        if t == 2:
            act(V("pk", 24, 96), V("df", 24, 96), Fn.Relu, scale=-1.0)
            ts(V("pk", 0, 24), V(lm, 0, 24), float(OFF + C), Op.is_ge, unit[2], Op.mult)
        landed(t, "ah%d" % t, 2, [V(lq, LH, LH + A), V(ls, LH, LH + A)])
        for bank in (1, 4, 3, 6, 0, 2):
            mm(bank, QE, 128 * (bank % 4), (lq, ls), LH - 32, 128)
        for q, b in (("m", 1), ("v", 1), ("a", 0), ("m", 3), ("v", 3), ("a", 2), ("m", 0), ("m", 2)):
            bank = b + 4 * (q == "a")
            d = V("ps", 512 * bank + 32, 512 * bank + 128)
            if q == "m":
                tt(V(win, DH + 4 * span + b, DH + 4 * (span + A), 4), d, V("oh", b, 4 * A, 4), Op.add)
            else:
                move(q, V(win, DH + b, DH + 4 * A, 4), d, 2.0)
        if t + 1 < R:
            for b in range(4):
                move("v" if b < 2 else "a", V(nxt, b, 4 * C, 4), ind(whole, V("fo", NK * b, NK * b + NK)))
    runs = ((0, 14), (14, NK))

    def gather(i, b):
        k0, k1 = runs[i]
        move("v" if b < 2 - i else "a", V(nxt, 64 * k0 + b, 64 * k1, 4), ind(whole, V("fo", NK * b + k0, NK * b + k1)))

    def pack(i):
        a, z = 16 * runs[i][0], 16 * runs[i][1]
        quant(V("qx", a, z), V("sx", a, z), V(nxt, 4 * a, 4 * z))
        mm(i, ("qv", "sv"), 0, QX, a, z - a)
        dma("s", T.oc[:, 4 * a:4 * z], T.qx[:, a:z].bitcast(dt.uint8), [V("qx", a, z)], [])

    def result(i):
        a, z = 16 * runs[i][0], 16 * runs[i][1]
        cp(V("yt", a, z), V("ps", 512 * i, 512 * i + z - a))
        dma("s", T.y[:, a:z], T.yt[:, a:z], [V("yt", a, z)], [])

    def scales(q, ks):
        for k in ks:
            dma(q, T.osc[4 * k:4 * k + 4, :], T.sx[32 * k:32 * k + 4, :], [V("sx", 0, C)], [])
    tt(W(16, 48), V("pk", 0, 48), V("pk", 48, 96), Op.add)
    ts(recv, mf, float(OFF), Op.is_gt, 256 * ONE, Op.mult)
    for b in (0, 2, 3):
        gather(0, b)
    tt(W(16), W(16), W(17), Op.add)
    gather(0, 1)
    tt(W(16), W(16), recv, Op.min)
    pack(0)
    tt(W(14), W(14), W(16), Op.add)
    for b in range(4):
        gather(1, b)
    ts(V("wu", 0, NK), W(14), 1 / ONE, Op.mult)
    pack(1)
    act(V("ovr", 0, C), ind(V("tab", 0, 256), V("wu", 0, NK)), Fn.Copy)
    scales("s", (0, 1))
    result(0)
    scales("a", (2, 3))
    result(1)
    dma("a", T.ov[:], T.ovr[0:128:16, :], [V("ovr", 0, C)], [])
    emit()
